import numpy as np
import ml_dtypes


def mxq(x, axis, fmt="e4m3"):
    dtype, down = {"e4m3": (ml_dtypes.float8_e4m3fn, 7), "e5m2": (ml_dtypes.float8_e5m2, 14)}[fmt]
    v = np.moveaxis(np.asarray(x, np.float32).astype(ml_dtypes.bfloat16).astype(np.float64), axis, -1)
    blocks = v.reshape(v.shape[:-1] + (-1, 32))
    amax = np.abs(blocks).max(-1, keepdims=True)
    byte = np.maximum(np.where(amax > 0, np.frexp(amax)[1] - 1 + 127, 0) - down, 1)
    scale = np.exp2(byte - 127.0)
    codes = (blocks / scale).astype(np.float32).astype(dtype).astype(np.float64)
    return np.moveaxis((codes * scale).reshape(v.shape), -1, axis)


WIDE = False


def mx_kscale(k):
    if not WIDE:
        return np.ones(k)
    levels = np.array([10, -10, 5, -5, 0])
    if k % 512:
        return np.exp2(np.random.permutation(np.resize(levels, k // 32))).repeat(32)
    a = np.empty((k // 512, 16))
    for p in range(k // 512):
        a[p, :8] = np.random.permutation(np.resize(levels, 8))
        for g in range(8):
            far = levels[np.abs(levels - a[p, g]) >= 10]
            a[p, g + 8] = far[np.random.randint(len(far))]
    return np.exp2(a.ravel()).repeat(32)


BF16 = ml_dtypes.bfloat16


def bf(x):
    return np.asarray(x, np.float32).astype(BF16)


def f64(x):
    return np.asarray(x).astype(np.float64)


E2M1 = np.array([0.0, 0.5, 1.0, 1.5, 2.0, 3.0, 4.0, 6.0, -0.0, -0.5, -1.0, -1.5, -2.0, -3.0, -4.0, -6.0])


def pack_weight(w, fmt):
    k, n = w.shape
    w = f64(bf(w)).reshape(k // 32, 32, n)
    amax = np.abs(w).max(1)
    if fmt == "e4m3":
        byte = np.frexp(amax)[1] - 1 + 127 - 7
    else:
        mant, ex = np.frexp(amax / 6.0)
        byte = np.where(mant > 0.5, ex, ex - 1) + 127
    byte = np.clip(np.where(amax > 0, byte, 1), 1, 254)
    scaled = (w * np.exp2(127.0 - byte)[:, None, :]).reshape(k, n).astype(np.float32)
    by_word = np.ascontiguousarray(scaled.reshape(k // 512, 128, 4, n).transpose(0, 1, 3, 2))
    if fmt == "e4m3":
        words = by_word.astype(ml_dtypes.float8_e4m3fn).view(np.uint8)
    else:
        c = by_word.astype(ml_dtypes.float4_e2m1fn).view(np.uint8) & 0xF
        words = c[..., 0::2] | (c[..., 1::2] << 4)
    return np.ascontiguousarray(words), np.ascontiguousarray(byte.astype(np.uint8).reshape(k // 512, 16, n))


def unpack_weight(words, scales, fmt):
    g, p, n, _ = words.shape
    if fmt == "e4m3":
        vals = np.ascontiguousarray(words).view(ml_dtypes.float8_e4m3fn).astype(np.float64)
    else:
        nib = np.empty((g, p, n, 4), np.uint8)
        nib[..., 0::2] = words & 0xF
        nib[..., 1::2] = words >> 4
        vals = E2M1[nib]
    vals = vals * np.repeat(np.exp2(scales.astype(np.float64) - 127.0), 8, axis=1)[..., None]
    return vals.transpose(0, 1, 3, 2).reshape(g * 512, n)
def pack4(w):
    words, scales = pack_weight(w, "e2m1")
    return words.reshape(words.shape[0], 128, -1), scales


def unpack4(words, scales):
    return unpack_weight(words.reshape(words.shape[0], 128, -1, 2), scales, "e2m1")


def planes(Y):
    n, m = Y.shape
    b = f64(bf(Y)).reshape(n // 32, 32, m)
    amax = np.abs(b).max(1)
    byte = np.clip(np.where(amax > 0, np.frexp(amax)[1] - 1 + 127 - 7, 1), 1, 254)
    codes = (b * np.exp2(127.0 - byte)[:, None, :]).reshape(n, m).astype(np.float32).astype(ml_dtypes.float8_e4m3fn).view(np.uint8)
    words = codes.reshape(n // 512, 128, 4, m).transpose(0, 1, 3, 2)
    return np.ascontiguousarray(words), np.ascontiguousarray(byte.astype(np.uint8).reshape(n // 512, 16, m))


T, P, D, F = 4, 256, 1024, 1024

def relu(v):
    return np.maximum(v, 0.0)

def setup_inputs():
    s = mx_kscale(D)
    t = mx_kscale(F)
    x = np.random.randn(D, T * P) * s[:, None]
    w1 = np.random.randn(D, T, F) / np.sqrt(D) / s[:, None, None] * t
    x_words, x_scales = pack_weight(x, "e4m3")
    w1_words, w1_scales = pack4(w1.reshape(D, T * F))
    w2 = np.random.randn(T, F, D) * np.sqrt(2.0 / F) / t[:, None]
    spread = np.exp(0.8 * np.random.randn(T, D))
    return {
        "x_words": x_words, "x_scales": x_scales,
        "w1_words": w1_words, "w1_scales": w1_scales,
        "b1": bf(0.3 * np.random.randn(T, F) * t),
        "w2": bf(w2),
        "b2": bf(0.3 * np.random.randn(T, D)),
        "gain": bf(spread),
        "skip": bf(0.7 * np.random.randn(T, P, D) * spread[:, None, :]),
    }

def reference(x_words, x_scales, w1_words, w1_scales, b1, w2, b2, gain, skip):
    X = unpack_weight(x_words, x_scales, "e4m3").T.reshape(T, P, D)
    W1 = unpack4(w1_words, w1_scales).reshape(D, T, F).transpose(1, 0, 2)
    h = relu((X @ W1) + f64(b1)[:, None, :])
    z = relu((mxq(h, 2, "e4m3") @ mxq(f64(w2), 1, "e4m3")) + f64(b2)[:, None, :])
    y = f64(skip) + f64(gain)[:, None, :] * z
    Y = y.reshape(T * P, D).T
    words, scales = planes(Y)
    return y, words, scales

@@ -1,0 +1,577 @@
+from contextlib import ExitStack
+
+import concourse.mybir as mybir
+from concourse.masks import make_identity
+
+F32 = mybir.dt.float32
+BF16 = mybir.dt.bfloat16
+I32 = mybir.dt.int32
+U32 = mybir.dt.uint32
+U8 = mybir.dt.uint8
+FP8X4 = mybir.dt.float8_e4m3fn_x4
+FP4X4 = mybir.dt.float4_e2m1fn_x4
+ALU = mybir.AluOpType
+ACT = mybir.ActivationFunctionType
+
+NETS, TOK, D, F = 4, 256, 1024, 1024
+FLOPS = 2 * NETS * TOK * D * F * 2
+P = 128
+HALF = 512
+UNITS = 2 * NETS
+VCOLS = 288
+NGRP = 3
+NWQ = 8
+NY = 6
+NRAW = 6
+NHQ = 4
+FAST = True
+WA = 3
+
+
+def tile_mask_hypernetwork_trunk_h2_kernel(
+    tc, x_words, x_scales, w1_words, w1_scales, b1, w2, b2, gain, skip, out_0, out_1, out_2
+):
+    nc = tc.nc
+    with ExitStack() as ctx:
+        sb = ctx.enter_context(tc.tile_pool(name="sb", bufs=1))
+        ps = ctx.enter_context(tc.psum_pool(name="ps", bufs=1))
+        ctx.enter_context(tc.manual_schedule())
+
+        def tiles(name, count, shape, dtype):
+            return [sb.tile(shape, dtype, name="%s%d" % (name, n), align_bytes=64) for n in range(count)]
+
+        def banks(name, count):
+            return [ps.tile([P, HALF], F32, name="%s%d" % (name, n)) for n in range(count)]
+
+        (ident,) = tiles("ident", 1, [P, P], F32)
+        (vec_bf,) = tiles("vec_bf", 1, [64, P], BF16)
+        (vec_rows,) = tiles("vec_rows", 1, [P, P], F32)
+        (vec_cols,) = tiles("vec_cols", 1, [P, 80], F32)
+        b1_all = tiles("b1_all", NETS, [P, HALF], F32)
+        (x_codes,) = tiles("x_codes", 1, [P, 2, NETS * TOK], U32)
+        (x_sc,) = tiles("x_sc", 1, [P, 2, NETS * TOK], U8)
+        w1_codes = tiles("w1_codes", NETS, [P, 2, 2 * F], U8)
+        (w1_sc_first,) = tiles("w1_sc_first", 1, [P, 2, F], U8)
+        (w1_sc_rest,) = tiles("w1_sc_rest", 1, [P, 2, (NETS - 1) * F], U8)
+        w2_raw = tiles("w2_raw", NRAW, [P, 4, D], BF16)
+        skip_sb = tiles("skip_sb", NETS, [P, 2, D], BF16)
+        w2_grp = tiles("w2_grp", NGRP, [P, HALF, 4], BF16)
+        w2_codes = tiles("w2_codes", NWQ, [P, 2, HALF], U32)
+        w2_sc = tiles("w2_sc", NWQ, [P, 2, HALF], U8)
+        h_rows = tiles("h_rows", 2, [P, 2, HALF], BF16)
+        h_grp = tiles("h_grp", 2, [P, 4 * TOK], BF16)
+        h_codes = tiles("h_codes", NHQ, [P, 2, TOK], U32)
+        h_sc = tiles("h_sc", NHQ, [P, 2, TOK], U8)
+        z_cols = tiles("z_cols", 2, [P, 4, TOK], F32)
+        y_rows = tiles("y_rows", NY, [P, 2, HALF], F32)
+        y_bf = tiles("y_bf", 2, [P, 2, HALF], BF16)
+        y_grp = tiles("y_grp", 2, [P, 2 * TOK], F32)
+        (y_codes,) = tiles("y_codes", 1, [P, 2, NETS * TOK], U32)
+        (y_sc,) = tiles("y_sc", 1, [P, 2, NETS * TOK], U8)
+
+        h_bank = banks("h_bank", 2)
+        (ht_bank,) = banks("ht_bank", 1)
+        z_bank = banks("z_bank", 2)
+        zt_bank = banks("zt_bank", 2)
+        (yt_bank,) = banks("yt_bank", 1)
+
+        def load_w2(i, g, c0, c1):
+            rows = w2[i, g * HALF : (g + 1) * HALF, :].rearrange("(p j) d -> p j d", j=4)
+            nc.sync.dma_start(out=w2_raw[(2 * i + g) % NRAW][:, :, c0:c1], in_=rows[:, :, c0:c1])
+
+        def load_scales(plane, src, c0, c1):
+            rows = src.rearrange("g q n -> q g n")
+            for quad in range(4):
+                nc.sync.dma_start(
+                    out=plane[32 * quad : 32 * quad + 4, :, :].bitcast(I32),
+                    in_=rows[4 * quad : 4 * quad + 4, :, c0:c1].bitcast(I32),
+                )
+
+        def load_x(c0, c1):
+            words = x_words.rearrange("g p n t -> p g (n t)")
+            nc.sync.dma_start(out=x_codes[:, :, c0:c1].bitcast(I32), in_=words[:, :, 4 * c0 : 4 * c1].bitcast(I32))
+
+        def load_w1(i):
+            words = w1_words.rearrange("g p n -> p g n")
+            nc.sync.dma_start(
+                out=w1_codes[i][:].bitcast(I32), in_=words[:, :, 2 * F * i : 2 * F * (i + 1)].bitcast(I32)
+            )
+
+        def load_skip(i):
+            nc.sync.dma_start(out=skip_sb[i][:], in_=skip[i].rearrange("(tt p) d -> p tt d", p=P))
+
+        def zero(tile):
+            nc.vector.memset(tile[:].bitcast(I32), 0)
+
+        def identity():
+            make_identity(nc, ident[:])
+
+        def vectors():
+            nc.vector.memset(vec_rows[:], 0.0)
+            nc.scalar.dma_start(out=vec_bf[0:32, :], in_=b2.rearrange("t (c n) -> (t c) n", n=P))
+            nc.scalar.dma_start(out=vec_bf[32:64, :], in_=gain.rearrange("t (c n) -> (t c) n", n=P))
+            nc.scalar.dma_start(out=vec_rows[64:80, :].bitcast(BF16), in_=b1.rearrange("t (c n) -> (t c) n", n=2 * P))
+
+        def turn_vectors():
+            nc.scalar.activation(out=vec_rows[0:64, :], in_=vec_bf[:], func=ACT.Identity)
+            nc.tensor.transpose(yt_bank[:, 0:P], vec_rows[:], ident[:])
+            nc.scalar.copy(out=vec_cols[:], in_=yt_bank[:, 0:80])
+
+        def spread_b1(i):
+            bank = (zt_bank + z_bank)[i]
+            for c in range(4):
+                col = vec_cols[:, 64 + 4 * i + c : 65 + 4 * i + c]
+                nc.tensor.transpose(bank[:, c * P : (c + 1) * P], col.to_broadcast([P, P]), ident[:])
+            nc.scalar.copy(out=b1_all[i][:], in_=bank[:])
+
+        def il_views(k, c0, c1):
+            unit, g = divmod(k, 2)
+            i, h = divmod(unit, 2)
+            src = w2_raw[(2 * i + g) % NRAW][:, :, h * HALF + c0 : h * HALF + c1]
+            dst = w2_grp[k % NGRP][:, c0:c1, :]
+            if FAST:
+                return dst.rearrange("p (c i) t -> p c t i", i=4), src.rearrange("p t (c i) -> p c t i", i=4)
+            return dst, src.rearrange("p t c -> p c t")
+
+        def il_v(k, c):
+            if 0 <= k < 2 * UNITS:
+                dst, src = il_views(k, 0, c)
+                nc.vector.tensor_copy(out=dst, in_=src)
+
+        def il_s(k, c):
+            if 0 <= k < 2 * UNITS:
+                dst, src = il_views(k, c, HALF)
+                nc.scalar.copy(out=dst, in_=src)
+
+        def q_w(k):
+            if 0 <= k < 2 * UNITS:
+                unit, g = divmod(k, 2)
+                nc.vector.quantize_mx(
+                    out=w2_codes[unit % NWQ][:, g, :].bitcast(FP8X4),
+                    scales=w2_sc[unit % NWQ][:, g, :],
+                    in_=w2_grp[k % NGRP][:].rearrange("p c t -> p (c t)"),
+                )
+
+        def mm1(q, tt):
+            if 0 <= q < UNITS:
+                i, fh = divmod(q, 2)
+                t0 = i * TOK + tt * P
+                plane, f0 = (w1_sc_first, fh * HALF) if i == 0 else (w1_sc_rest, (i - 1) * F + fh * HALF)
+                for g in range(2):
+                    nc.tensor.matmul_mx(
+                        out=h_bank[tt][:],
+                        lhsT=x_codes[:, g, t0 : t0 + P].bitcast(FP8X4),
+                        lhsT_scale=x_sc[:, g, t0 : t0 + P],
+                        rhs=w1_codes[i][:, g, 2 * fh * HALF : 2 * (fh + 1) * HALF].bitcast(FP4X4),
+                        rhs_scale=plane[:, g, f0 : f0 + HALF],
+                        start=(g == 0),
+                        stop=(g == 1),
+                    )
+
+        def add_b1(q, tt):
+            if 0 <= q < UNITS:
+                i, fh = divmod(q, 2)
+                nc.vector.tensor_tensor(
+                    out=h_rows[q % 2][:, tt, :],
+                    in0=h_bank[tt][:],
+                    in1=b1_all[i][:].bitcast(BF16)[:, fh * HALF : (fh + 1) * HALF],
+                    op=ALU.add,
+                )
+
+        def turn_words(bank, rows):
+            for tt in range(2):
+                words = rows[:, tt, :].bitcast(F32)
+                for u in range(2):
+                    c0 = u * TOK + tt * P
+                    nc.tensor.transpose(bank[:, c0 : c0 + P], words[:, u : 2 * P : 2], ident[:])
+
+        def turn_h(q):
+            if 0 <= q < UNITS:
+                turn_words(ht_bank, h_rows[q % 2])
+
+        def relu_h(q):
+            if 0 <= q < UNITS:
+                nc.scalar.activation(
+                    out=h_grp[q % 2][:].rearrange("p (r u e) -> p r u e", u=2, e=2),
+                    in_=ht_bank[:].bitcast(BF16).rearrange("p (u r e) -> p r u e", u=2, e=2),
+                    func=ACT.Relu,
+                )
+
+        def q_h(q):
+            if 0 <= q < UNITS:
+                i, fh = divmod(q, 2)
+                nc.vector.quantize_mx(
+                    out=h_codes[i % NHQ][:, fh, :].bitcast(FP8X4), scales=h_sc[i % NHQ][:, fh, :], in_=h_grp[q % 2][:]
+                )
+
+        def mm2(p, z):
+            if 0 <= p < UNITS:
+                i = p // 2
+                for dl in range(2):
+                    d0 = (2 * z + dl) * P
+                    for g in range(2):
+                        nc.tensor.matmul_mx(
+                            out=z_bank[z][:, dl * TOK : (dl + 1) * TOK],
+                            lhsT=w2_codes[p % NWQ][:, g, d0 : d0 + P].bitcast(FP8X4),
+                            lhsT_scale=w2_sc[p % NWQ][:, g, d0 : d0 + P],
+                            rhs=h_codes[i % NHQ][:, g, :].bitcast(FP8X4),
+                            rhs_scale=h_sc[i % NHQ][:, g, :],
+                            start=(g == 0),
+                            stop=(g == 1),
+                        )
+
+        def relu_z(p, z):
+            if 0 <= p < UNITS:
+                for dl in range(2):
+                    c = 4 * p + 2 * z + dl
+                    nc.scalar.activation(
+                        out=z_cols[p % 2][:, 2 * z + dl, :],
+                        in_=z_bank[z][:, dl * TOK : (dl + 1) * TOK],
+                        func=ACT.Relu,
+                        bias=vec_cols[:, c : c + 1],
+                    )
+
+        def mul_gain(p, z):
+            if 0 <= p < UNITS:
+                for dl in range(2):
+                    c = 32 + 4 * p + 2 * z + dl
+                    zc = z_cols[p % 2][:, 2 * z + dl, :]
+                    nc.vector.tensor_scalar(
+                        out=zc, in0=zc, scalar1=vec_cols[:, c : c + 1], scalar2=None, op0=ALU.mult
+                    )
+
+        def turn_z(p, z):
+            if 0 <= p < UNITS:
+                for tt in range(2):
+                    for dl in range(2):
+                        c0 = tt * TOK + dl * P
+                        nc.tensor.transpose(
+                            zt_bank[z][:, c0 : c0 + P], z_cols[p % 2][:, 2 * z + dl, tt * P : (tt + 1) * P], ident[:]
+                        )
+
+        def add_skip(p, z):
+            if 0 <= p < UNITS:
+                i, h = divmod(p, 2)
+                d0 = h * HALF + z * 256
+                nc.vector.tensor_tensor(
+                    out=y_rows[p % NY][:, :, z * 256 : (z + 1) * 256],
+                    in0=zt_bank[z][:].rearrange("p (tt d) -> p tt d", tt=2),
+                    in1=skip_sb[i][:, :, d0 : d0 + 256],
+                    op=ALU.add,
+                )
+
+        def store_y(p):
+            if 0 <= p < UNITS:
+                i, h = divmod(p, 2)
+                dst = out_0[i].rearrange("(tt p) d -> p tt d", p=P)[:, :, h * HALF : (h + 1) * HALF]
+                nc.sync.dma_start(out=dst, in_=y_rows[p % NY][:])
+
+        def cast_y(p):
+            if 0 <= p < UNITS:
+                nc.scalar.copy(out=y_bf[p % 2][:], in_=y_rows[p % NY][:])
+
+        def cast_y_v(p):
+            if 0 <= p < UNITS:
+                nc.vector.tensor_copy(out=y_bf[p % 2][:], in_=y_rows[p % NY][:])
+
+        def turn_y(p):
+            if 0 <= p < UNITS:
+                turn_words(yt_bank, y_bf[p % 2])
+
+        def copy_y(p):
+            if 0 <= p < UNITS:
+                nc.scalar.copy(
+                    out=y_grp[p % 2][:].rearrange("p (r u) -> p r u", u=2),
+                    in_=yt_bank[:].rearrange("p (u r) -> p r u", u=2),
+                )
+
+        def q_y(p):
+            if 0 <= p < UNITS:
+                i, h = divmod(p, 2)
+                cols = slice(i * TOK, (i + 1) * TOK)
+                nc.vector.quantize_mx(
+                    out=y_codes[:, h, cols].bitcast(FP8X4), scales=y_sc[:, h, cols], in_=y_grp[p % 2][:].bitcast(BF16)
+                )
+
+        def store_codes(p):
+            if 0 <= p < UNITS:
+                i, h = divmod(p, 2)
+                dst = out_1[h].rearrange("p m t -> p (m t)")[:, 4 * i * TOK : 4 * (i + 1) * TOK]
+                nc.sync.dma_start(out=dst.bitcast(I32), in_=y_codes[:, h, i * TOK : (i + 1) * TOK].bitcast(I32))
+
+        def store_scales(c0, c1):
+            rows = out_2.rearrange("g q m -> q g m")
+            for quad in range(4):
+                nc.sync.dma_start(
+                    out=rows[4 * quad : 4 * quad + 4, :, c0:c1].bitcast(I32),
+                    in_=y_sc[32 * quad : 32 * quad + 4, :, c0:c1].bitcast(I32),
+                )
+
+        identity()
+        vectors()
+        zero(x_sc)
+        zero(w1_sc_first)
+        zero(w1_sc_rest)
+        load_x(256, 512)
+        load_w1(0)
+        load_scales(w1_sc_first, w1_scales, 0, 1024)
+        load_w2(0, 0, 0, 512)
+        load_scales(x_sc, x_scales, 0, 1024)
+        load_x(0, 256)
+        load_scales(w1_sc_rest, w1_scales, 1024, 4096)
+        load_w2(0, 1, 0, 512)
+        load_w2(0, 0, 512, 1024)
+        load_w1(1)
+        load_w2(0, 1, 512, 1024)
+        load_w2(1, 0, 0, 1024)
+        load_w2(1, 1, 0, 1024)
+        load_w1(2)
+        load_x(512, 1024)
+        load_w2(2, 0, 0, 1024)
+        load_skip(0)
+        load_w1(3)
+        load_skip(1)
+        load_w2(2, 1, 0, 1024)
+        load_skip(2)
+        turn_vectors()
+        spread_b1(0)
+        spread_b1(1)
+        spread_b1(2)
+        spread_b1(3)
+        mm1(0, 0)
+        add_b1(0, 0)
+        mm1(0, 1)
+        add_b1(0, 1)
+        mm1(1, 0)
+        il_s(0, 288)
+        il_v(0, 288)
+        add_b1(1, 0)
+        q_w(0)
+        turn_h(0)
+        mm1(1, 1)
+        add_b1(1, 1)
+        relu_h(0)
+        il_s(1, 288)
+        mm1(2, 0)
+        il_s(2, 288)
+        q_h(0)
+        il_v(1, 288)
+        il_v(2, 288)
+        add_b1(2, 0)
+        q_w(2)
+        turn_h(1)
+        q_w(1)
+        mm1(2, 1)
+        add_b1(2, 1)
+        relu_h(1)
+        il_s(3, 288)
+        mm1(3, 0)
+        il_s(4, 288)
+        q_h(1)
+        il_v(3, 288)
+        load_w2(3, 0, 0, 1024)
+        load_w2(3, 1, 0, 1024)
+        load_skip(3)
+        il_v(4, 288)
+        add_b1(3, 0)
+        mm2(0, 0)
+        q_w(4)
+        relu_z(0, 0)
+        turn_h(2)
+        q_w(3)
+        mm1(3, 1)
+        add_b1(3, 1)
+        mm2(0, 1)
+        relu_h(2)
+        il_s(5, 288)
+        mm1(4, 0)
+        il_s(6, 288)
+        q_h(2)
+        il_v(5, 288)
+        il_v(6, 288)
+        add_b1(4, 0)
+        relu_z(0, 1)
+        mm2(1, 0)
+        q_w(6)
+        mul_gain(0, 0)
+        relu_z(1, 0)
+        turn_h(3)
+        q_w(5)
+        mm1(4, 1)
+        mul_gain(0, 1)
+        add_b1(4, 1)
+        mm2(1, 1)
+        relu_h(3)
+        il_s(7, 288)
+        mm1(5, 0)
+        il_s(8, 288)
+        q_h(3)
+        il_v(7, 288)
+        turn_z(0, 0)
+        il_v(8, 288)
+        add_b1(5, 0)
+        relu_z(1, 1)
+        turn_z(0, 1)
+        mm2(2, 0)
+        add_skip(0, 0)
+        q_w(8)
+        mul_gain(1, 0)
+        relu_z(2, 0)
+        turn_h(4)
+        q_w(7)
+        mm1(5, 1)
+        mul_gain(1, 1)
+        add_b1(5, 1)
+        mm2(2, 1)
+        add_skip(0, 1)
+        relu_h(4)
+        il_s(9, 288)
+        mm1(6, 0)
+        il_s(10, 288)
+        q_h(4)
+        il_v(9, 288)
+        turn_z(1, 0)
+        il_v(10, 288)
+        add_b1(6, 0)
+        relu_z(2, 1)
+        turn_z(1, 1)
+        mm2(3, 0)
+        cast_y(0)
+        add_skip(1, 0)
+        q_w(10)
+        mul_gain(2, 0)
+        relu_z(3, 0)
+        turn_h(5)
+        q_w(9)
+        mm1(6, 1)
+        mul_gain(2, 1)
+        add_b1(6, 1)
+        mm2(3, 1)
+        add_skip(1, 1)
+        relu_h(5)
+        il_s(11, 288)
+        mm1(7, 0)
+        il_s(12, 288)
+        q_h(5)
+        il_v(11, 288)
+        turn_z(2, 0)
+        il_v(12, 288)
+        add_b1(7, 0)
+        relu_z(3, 1)
+        turn_y(0)
+        turn_z(2, 1)
+        mm2(4, 0)
+        copy_y(0)
+        cast_y(1)
+        add_skip(2, 0)
+        q_w(12)
+        mul_gain(3, 0)
+        relu_z(4, 0)
+        turn_h(6)
+        q_w(11)
+        mm1(7, 1)
+        mul_gain(3, 1)
+        add_b1(7, 1)
+        mm2(4, 1)
+        add_skip(2, 1)
+        relu_h(6)
+        il_s(13, 288)
+        il_s(14, 288)
+        q_h(6)
+        il_v(13, 288)
+        turn_z(3, 0)
+        il_v(14, 288)
+        relu_z(4, 1)
+        turn_y(1)
+        turn_z(3, 1)
+        mm2(5, 0)
+        store_y(0)
+        copy_y(1)
+        q_y(0)
+        cast_y(2)
+        add_skip(3, 0)
+        q_w(14)
+        mul_gain(4, 0)
+        relu_z(5, 0)
+        turn_h(7)
+        q_w(13)
+        mul_gain(4, 1)
+        mm2(5, 1)
+        add_skip(3, 1)
+        relu_h(7)
+        il_s(15, 288)
+        q_h(7)
+        il_v(15, 288)
+        turn_z(4, 0)
+        relu_z(5, 1)
+        turn_y(2)
+        turn_z(4, 1)
+        mm2(6, 0)
+        store_y(1)
+        copy_y(2)
+        q_y(1)
+        cast_y(3)
+        add_skip(4, 0)
+        mul_gain(5, 0)
+        relu_z(6, 0)
+        q_w(15)
+        mul_gain(5, 1)
+        store_codes(0)
+        mm2(6, 1)
+        add_skip(4, 1)
+        turn_z(5, 0)
+        relu_z(6, 1)
+        turn_y(3)
+        turn_z(5, 1)
+        mm2(7, 0)
+        store_y(2)
+        copy_y(3)
+        q_y(2)
+        cast_y(4)
+        add_skip(5, 0)
+        mul_gain(6, 0)
+        relu_z(7, 0)
+        mul_gain(6, 1)
+        store_codes(1)
+        mm2(7, 1)
+        add_skip(5, 1)
+        turn_z(6, 0)
+        relu_z(7, 1)
+        turn_y(4)
+        turn_z(6, 1)
+        store_y(3)
+        copy_y(4)
+        q_y(3)
+        cast_y_v(5)
+        add_skip(6, 0)
+        mul_gain(7, 0)
+        mul_gain(7, 1)
+        store_codes(2)
+        add_skip(6, 1)
+        turn_z(7, 0)
+        turn_y(5)
+        turn_z(7, 1)
+        store_y(4)
+        copy_y(5)
+        q_y(4)
+        cast_y_v(6)
+        add_skip(7, 0)
+        store_codes(3)
+        add_skip(7, 1)
+        turn_y(6)
+        store_y(5)
+        copy_y(6)
+        q_y(5)
+        cast_y_v(7)
+        store_codes(4)
+        turn_y(7)
+        store_y(6)
+        copy_y(7)
+        q_y(6)
+        store_codes(5)
+        store_scales(0, 768)
+        store_y(7)
+        q_y(7)
+        store_codes(6)
+        store_codes(7)
+        store_scales(768, 1024)

@@ -44,27 +44,27 @@ def tile_mask_hypernetwork_trunk_h2_kernel(
             return [ps.tile([P, HALF], F32, name="%s%d" % (name, n)) for n in range(count)]
 
         (ident,) = tiles("ident", 1, [P, P], F32)
-        (vec_bf,) = tiles("vec_bf", 1, [64, P], BF16)
+        (ident_bf,) = tiles("ident_bf", 1, [P, P], BF16)
+        (vec_bf,) = tiles("vec_bf", 1, [96, P], BF16)
         (vec_rows,) = tiles("vec_rows", 1, [P, P], F32)
-        (vec_cols,) = tiles("vec_cols", 1, [P, 80], F32)
-        b1_all = tiles("b1_all", NETS, [P, HALF], F32)
+        (vec_cols,) = tiles("vec_cols", 1, [P, 96], F32)
         (x_codes,) = tiles("x_codes", 1, [P, 2, NETS * TOK], U32)
         (x_sc,) = tiles("x_sc", 1, [P, 2, NETS * TOK], U8)
         w1_codes = tiles("w1_codes", NETS, [P, 2, 2 * F], U8)
-        (w1_sc_first,) = tiles("w1_sc_first", 1, [P, 2, F], U8)
-        (w1_sc_rest,) = tiles("w1_sc_rest", 1, [P, 2, (NETS - 1) * F], U8)
+        (w1_sc,) = tiles("w1_sc", 1, [P, 2, NETS * F], U8)
         w2_raw = tiles("w2_raw", NRAW, [P, 4, D], BF16)
         skip_sb = tiles("skip_sb", NETS, [P, 2, D], BF16)
         w2_grp = tiles("w2_grp", NGRP, [P, HALF, 4], BF16)
         w2_codes = tiles("w2_codes", NWQ, [P, 2, HALF], U32)
         w2_sc = tiles("w2_sc", NWQ, [P, 2, HALF], U8)
-        h_rows = tiles("h_rows", 2, [P, 2, HALF], BF16)
-        h_grp = tiles("h_grp", 2, [P, 4 * TOK], BF16)
+        h_rows = tiles("h_rows", 2, [P, 2, 2, 2 * P], BF16)
+        h_cols = tiles("h_cols", 2, [P, 4, TOK], BF16)
+        h_grp = tiles("h_grp", 2, [P, 2 * TOK], F32)
         h_codes = tiles("h_codes", NHQ, [P, 2, TOK], U32)
         h_sc = tiles("h_sc", NHQ, [P, 2, TOK], U8)
         z_cols = tiles("z_cols", 2, [P, 4, TOK], F32)
         y_rows = tiles("y_rows", NY, [P, 2, HALF], F32)
-        y_bf = tiles("y_bf", 2, [P, 2, HALF], BF16)
+        y_bf = tiles("y_bf", 2, [P, 2, 2, 2 * P], BF16)
         y_grp = tiles("y_grp", 2, [P, 2 * TOK], F32)
         (y_codes,) = tiles("y_codes", 1, [P, 2, NETS * TOK], U32)
         (y_sc,) = tiles("y_sc", 1, [P, 2, NETS * TOK], U8)
@@ -73,7 +73,7 @@ def tile_mask_hypernetwork_trunk_h2_kernel(
         (ht_bank,) = banks("ht_bank", 1)
         z_bank = banks("z_bank", 2)
         zt_bank = banks("zt_bank", 2)
-        (yt_bank,) = banks("yt_bank", 1)
+        (word_bank,) = banks("word_bank", 1)
 
         def load_w2(i, g, c0, c1):
             rows = w2[i, g * HALF : (g + 1) * HALF, :].rearrange("(p j) d -> p j d", j=4)
@@ -83,7 +83,7 @@ def tile_mask_hypernetwork_trunk_h2_kernel(
             rows = src.rearrange("g q n -> q g n")
             for quad in range(4):
                 nc.sync.dma_start(
-                    out=plane[32 * quad : 32 * quad + 4, :, :].bitcast(I32),
+                    out=plane[32 * quad : 32 * quad + 4, :, c0:c1].bitcast(I32),
                     in_=rows[4 * quad : 4 * quad + 4, :, c0:c1].bitcast(I32),
                 )
 
@@ -100,29 +100,29 @@ def tile_mask_hypernetwork_trunk_h2_kernel(
         def load_skip(i):
             nc.sync.dma_start(out=skip_sb[i][:], in_=skip[i].rearrange("(tt p) d -> p tt d", p=P))
 
-        def zero(tile):
-            nc.vector.memset(tile[:].bitcast(I32), 0)
+        def zero(plane, c0, c1):
+            nc.vector.memset(plane[:, :, c0:c1].bitcast(I32), 0)
 
         def identity():
             make_identity(nc, ident[:])
+            make_identity(nc, ident_bf[:])
 
-        def vectors():
+        def vec_zero():
             nc.vector.memset(vec_rows[:], 0.0)
+
+        def vec_load():
             nc.scalar.dma_start(out=vec_bf[0:32, :], in_=b2.rearrange("t (c n) -> (t c) n", n=P))
             nc.scalar.dma_start(out=vec_bf[32:64, :], in_=gain.rearrange("t (c n) -> (t c) n", n=P))
-            nc.scalar.dma_start(out=vec_rows[64:80, :].bitcast(BF16), in_=b1.rearrange("t (c n) -> (t c) n", n=2 * P))
+            nc.scalar.dma_start(out=vec_bf[64:96, :], in_=b1.rearrange("t (c n) -> (t c) n", n=P))
 
-        def turn_vectors():
-            nc.scalar.activation(out=vec_rows[0:64, :], in_=vec_bf[:], func=ACT.Identity)
-            nc.tensor.transpose(yt_bank[:, 0:P], vec_rows[:], ident[:])
-            nc.scalar.copy(out=vec_cols[:], in_=yt_bank[:, 0:80])
+        def vec_cast():
+            nc.scalar.activation(out=vec_rows[0:96, :], in_=vec_bf[:], func=ACT.Identity)
 
-        def spread_b1(i):
-            bank = (zt_bank + z_bank)[i]
-            for c in range(4):
-                col = vec_cols[:, 64 + 4 * i + c : 65 + 4 * i + c]
-                nc.tensor.transpose(bank[:, c * P : (c + 1) * P], col.to_broadcast([P, P]), ident[:])
-            nc.scalar.copy(out=b1_all[i][:], in_=bank[:])
+        def vec_turn():
+            nc.tensor.transpose(word_bank[:, 0:P], vec_rows[:], ident[:])
+
+        def vec_copy():
+            nc.scalar.copy(out=vec_cols[:], in_=word_bank[:, 0:96])
 
         def il_views(k, c0, c1):
             unit, g = divmod(k, 2)
@@ -138,10 +138,15 @@ def tile_mask_hypernetwork_trunk_h2_kernel(
                 dst, src = il_views(k, 0, c)
                 nc.vector.tensor_copy(out=dst, in_=src)
 
-        def il_s(k, c):
+        def il_s(k, c, c1=HALF):
+            if c < c1:
+                dst, src = il_views(k, c, c1)
+                nc.scalar.copy(out=dst, in_=src)
+
+        def il_p(k, c):
             if 0 <= k < 2 * UNITS:
                 dst, src = il_views(k, c, HALF)
-                nc.scalar.copy(out=dst, in_=src)
+                nc.gpsimd.tensor_scalar(out=dst, in0=src, scalar1=1.0, scalar2=0.0, op0=ALU.mult, op1=ALU.add)
 
         def q_w(k):
             if 0 <= k < 2 * UNITS:
@@ -152,56 +157,82 @@ def tile_mask_hypernetwork_trunk_h2_kernel(
                     in_=w2_grp[k % NGRP][:].rearrange("p c t -> p (c t)"),
                 )
 
-        def mm1(q, tt):
+        def mm1(q, s):
             if 0 <= q < UNITS:
                 i, fh = divmod(q, 2)
-                t0 = i * TOK + tt * P
-                plane, f0 = (w1_sc_first, fh * HALF) if i == 0 else (w1_sc_rest, (i - 1) * F + fh * HALF)
-                for g in range(2):
-                    nc.tensor.matmul_mx(
-                        out=h_bank[tt][:],
-                        lhsT=x_codes[:, g, t0 : t0 + P].bitcast(FP8X4),
-                        lhsT_scale=x_sc[:, g, t0 : t0 + P],
-                        rhs=w1_codes[i][:, g, 2 * fh * HALF : 2 * (fh + 1) * HALF].bitcast(FP4X4),
-                        rhs_scale=plane[:, g, f0 : f0 + HALF],
-                        start=(g == 0),
-                        stop=(g == 1),
+                for fl in range(2):
+                    f0 = fh * HALF + (2 * s + fl) * P
+                    for tt in range(2):
+                        t0 = i * TOK + tt * P
+                        c0 = fl * TOK + tt * P
+                        for g in range(2):
+                            nc.tensor.matmul_mx(
+                                out=h_bank[s][:, c0 : c0 + P],
+                                lhsT=w1_codes[i][:, g, 2 * f0 : 2 * (f0 + P)].bitcast(FP4X4),
+                                lhsT_scale=w1_sc[:, g, i * F + f0 : i * F + f0 + P],
+                                rhs=x_codes[:, g, t0 : t0 + P].bitcast(FP8X4),
+                                rhs_scale=x_sc[:, g, t0 : t0 + P],
+                                start=(g == 0),
+                                stop=(g == 1),
+                            )
+
+        def relu_h(q, s):
+            if 0 <= q < UNITS:
+                for fl in range(2):
+                    c = 64 + 4 * q + 2 * s + fl
+                    nc.scalar.activation(
+                        out=h_cols[q % 2][:, 2 * s + fl, :],
+                        in_=h_bank[s][:, fl * TOK : (fl + 1) * TOK],
+                        func=ACT.Relu,
+                        bias=vec_cols[:, c : c + 1],
                     )
 
-        def add_b1(q, tt):
+        def rows_h(q):
             if 0 <= q < UNITS:
-                i, fh = divmod(q, 2)
-                nc.vector.tensor_tensor(
-                    out=h_rows[q % 2][:, tt, :],
-                    in0=h_bank[tt][:],
-                    in1=b1_all[i][:].bitcast(BF16)[:, fh * HALF : (fh + 1) * HALF],
-                    op=ALU.add,
+                for tt in range(2):
+                    for fl in range(4):
+                        c0 = tt * HALF + fl * P
+                        nc.tensor.transpose(
+                            ht_bank[:].bitcast(BF16)[:, c0 : c0 + P],
+                            h_cols[q % 2][:, fl, tt * P : (tt + 1) * P],
+                            ident_bf[:],
+                        )
+
+        def split_h(q):
+            if 0 <= q < UNITS:
+                nc.scalar.copy(
+                    out=h_rows[q % 2][:].rearrange("p u tt w -> p u (tt w)").bitcast(F32),
+                    in_=ht_bank[:].rearrange("p (w u) -> p u w", u=2),
                 )
 
         def turn_words(bank, rows):
             for tt in range(2):
-                words = rows[:, tt, :].bitcast(F32)
                 for u in range(2):
                     c0 = u * TOK + tt * P
-                    nc.tensor.transpose(bank[:, c0 : c0 + P], words[:, u : 2 * P : 2], ident[:])
+                    nc.tensor.transpose(bank[:, c0 : c0 + P], rows[:, u, tt, :].bitcast(F32), ident[:])
+
+        def split_h_v(q):
+            nc.vector.tensor_copy(
+                out=h_rows[q % 2][:].rearrange("p u tt w -> p u (tt w)").bitcast(F32),
+                in_=ht_bank[:].rearrange("p (w u) -> p u w", u=2),
+            )
 
         def turn_h(q):
             if 0 <= q < UNITS:
-                turn_words(ht_bank, h_rows[q % 2])
+                turn_words(word_bank, h_rows[q % 2])
 
-        def relu_h(q):
+        def copy_h(q):
             if 0 <= q < UNITS:
-                nc.scalar.activation(
-                    out=h_grp[q % 2][:].rearrange("p (r u e) -> p r u e", u=2, e=2),
-                    in_=ht_bank[:].bitcast(BF16).rearrange("p (u r e) -> p r u e", u=2, e=2),
-                    func=ACT.Relu,
+                nc.scalar.copy(
+                    out=h_grp[q % 2][:].rearrange("p (r u) -> p r u", u=2),
+                    in_=word_bank[:].rearrange("p (u r) -> p r u", u=2),
                 )
 
         def q_h(q):
             if 0 <= q < UNITS:
                 i, fh = divmod(q, 2)
                 nc.vector.quantize_mx(
-                    out=h_codes[i % NHQ][:, fh, :].bitcast(FP8X4), scales=h_sc[i % NHQ][:, fh, :], in_=h_grp[q % 2][:]
+                    out=h_codes[i % NHQ][:, fh, :].bitcast(FP8X4), scales=h_sc[i % NHQ][:, fh, :], in_=h_grp[q % 2][:].bitcast(BF16)
                 )
 
         def mm2(p, z):
@@ -240,6 +271,12 @@ def tile_mask_hypernetwork_trunk_h2_kernel(
                         out=zc, in0=zc, scalar1=vec_cols[:, c : c + 1], scalar2=None, op0=ALU.mult
                     )
 
+        def mul_gain_s(p, z):
+            for dl in range(2):
+                c = 32 + 4 * p + 2 * z + dl
+                zc = z_cols[p % 2][:, 2 * z + dl, :]
+                nc.scalar.activation(out=zc, in_=zc, func=ACT.Copy, scale=vec_cols[:, c : c + 1])
+
         def turn_z(p, z):
             if 0 <= p < UNITS:
                 for tt in range(2):
@@ -266,23 +303,29 @@ def tile_mask_hypernetwork_trunk_h2_kernel(
                 dst = out_0[i].rearrange("(tt p) d -> p tt d", p=P)[:, :, h * HALF : (h + 1) * HALF]
                 nc.sync.dma_start(out=dst, in_=y_rows[p % NY][:])
 
+        def cast_views(p):
+            dst = y_bf[p % 2][:].rearrange("p u tt (w e) -> p u (tt w) e", e=2)
+            return dst, y_rows[p % NY][:].rearrange("p tt (w u e) -> p u (tt w) e", u=2, e=2)
+
         def cast_y(p):
             if 0 <= p < UNITS:
-                nc.scalar.copy(out=y_bf[p % 2][:], in_=y_rows[p % NY][:])
+                dst, src = cast_views(p)
+                nc.scalar.copy(out=dst, in_=src)
 
         def cast_y_v(p):
             if 0 <= p < UNITS:
-                nc.vector.tensor_copy(out=y_bf[p % 2][:], in_=y_rows[p % NY][:])
+                dst, src = cast_views(p)
+                nc.vector.tensor_copy(out=dst, in_=src)
 
         def turn_y(p):
             if 0 <= p < UNITS:
-                turn_words(yt_bank, y_bf[p % 2])
+                turn_words(word_bank, y_bf[p % 2])
 
         def copy_y(p):
             if 0 <= p < UNITS:
                 nc.scalar.copy(
                     out=y_grp[p % 2][:].rearrange("p (r u) -> p r u", u=2),
-                    in_=yt_bank[:].rearrange("p (u r) -> p r u", u=2),
+                    in_=word_bank[:].rearrange("p (u r) -> p r u", u=2),
                 )
 
         def q_y(p):
@@ -308,270 +351,287 @@ def tile_mask_hypernetwork_trunk_h2_kernel(
                 )
 
         identity()
-        vectors()
-        zero(x_sc)
-        zero(w1_sc_first)
-        zero(w1_sc_rest)
-        load_x(256, 512)
+        vec_load()
+        zero(w1_sc, 0, 1024)
         load_w1(0)
-        load_scales(w1_sc_first, w1_scales, 0, 1024)
+        zero(w1_sc, 1024, 4096)
+        load_scales(w1_sc, w1_scales, 0, 1024)
+        vec_zero()
+        zero(x_sc, 0, 1024)
         load_w2(0, 0, 0, 512)
-        load_scales(x_sc, x_scales, 0, 1024)
         load_x(0, 256)
-        load_scales(w1_sc_rest, w1_scales, 1024, 4096)
+        load_scales(x_sc, x_scales, 0, 256)
+        vec_cast()
+        vec_turn()
         load_w2(0, 1, 0, 512)
-        load_w2(0, 0, 512, 1024)
-        load_w1(1)
         load_w2(0, 1, 512, 1024)
-        load_w2(1, 0, 0, 1024)
-        load_w2(1, 1, 0, 1024)
-        load_w1(2)
-        load_x(512, 1024)
-        load_w2(2, 0, 0, 1024)
-        load_skip(0)
-        load_w1(3)
-        load_skip(1)
-        load_w2(2, 1, 0, 1024)
-        load_skip(2)
-        turn_vectors()
-        spread_b1(0)
-        spread_b1(1)
-        spread_b1(2)
-        spread_b1(3)
+        vec_copy()
+        load_scales(w1_sc, w1_scales, 1024, 2048)
+        il_v(0, 320)
+        il_s(0, 320, 512)
+        load_w2(0, 0, 512, 1024)
         mm1(0, 0)
-        add_b1(0, 0)
-        mm1(0, 1)
-        add_b1(0, 1)
-        mm1(1, 0)
-        il_s(0, 288)
-        il_v(0, 288)
-        add_b1(1, 0)
+        load_scales(x_sc, x_scales, 256, 1024)
         q_w(0)
-        turn_h(0)
-        mm1(1, 1)
-        add_b1(1, 1)
-        relu_h(0)
-        il_s(1, 288)
-        mm1(2, 0)
-        il_s(2, 288)
-        q_h(0)
-        il_v(1, 288)
-        il_v(2, 288)
-        add_b1(2, 0)
-        q_w(2)
-        turn_h(1)
+        il_v(1, 496)
+        mm1(0, 1)
+        relu_h(0, 0)
+        il_v(3, 384)
+        mm1(1, 0)
+        load_x(256, 512)
+        load_w1(1)
+        relu_h(0, 1)
+        load_w2(1, 0, 0, 1024)
+        rows_h(0)
+        il_s(1, 496, 512)
+        il_s(3, 384, 512)
         q_w(1)
-        mm1(2, 1)
-        add_b1(2, 1)
-        relu_h(1)
-        il_s(3, 288)
-        mm1(3, 0)
-        il_s(4, 288)
-        q_h(1)
-        il_v(3, 288)
-        load_w2(3, 0, 0, 1024)
-        load_w2(3, 1, 0, 1024)
-        load_skip(3)
-        il_v(4, 288)
-        add_b1(3, 0)
-        mm2(0, 0)
-        q_w(4)
-        relu_z(0, 0)
-        turn_h(2)
+        mm1(1, 1)
+        load_scales(w1_sc, w1_scales, 2048, 4096)
+        relu_h(1, 0)
+        split_h_v(0)
+        load_w2(1, 1, 0, 1024)
+        il_v(2, 480)
+        relu_h(1, 1)
+        turn_h(0)
+        load_w1(2)
+        rows_h(1)
+        il_s(2, 480, 512)
+        copy_h(0)
         q_w(3)
+        load_skip(0)
+        split_h_v(1)
+        mm1(2, 0)
+        q_w(2)
+        q_h(0)
+        mm1(2, 1)
+        relu_h(2, 0)
+        turn_h(1)
+        load_x(512, 1024)
+        il_v(4, 496)
+        relu_h(2, 1)
+        load_w2(2, 0, 0, 1024)
+        mm1(3, 0)
+        load_w1(3)
+        copy_h(1)
+        load_skip(1)
+        rows_h(2)
+        relu_h(3, 0)
+        load_w2(2, 1, 0, 1024)
+        q_h(1)
         mm1(3, 1)
-        add_b1(3, 1)
-        mm2(0, 1)
-        relu_h(2)
-        il_s(5, 288)
-        mm1(4, 0)
-        il_s(6, 288)
-        q_h(2)
-        il_v(5, 288)
-        il_v(6, 288)
-        add_b1(4, 0)
-        relu_z(0, 1)
-        mm2(1, 0)
+        il_v(6, 496)
+        il_s(4, 496, 512)
+        split_h(2)
+        mm2(0, 0)
+        relu_h(3, 1)
+        turn_h(2)
+        q_w(4)
+        il_s(6, 496, 512)
+        rows_h(3)
+        relu_z(0, 0)
         q_w(6)
+        load_skip(2)
+        mm2(0, 1)
+        copy_h(2)
         mul_gain(0, 0)
-        relu_z(1, 0)
+        mm2(1, 0)
+        il_v(5, 432)
+        split_h(3)
+        load_w2(3, 0, 0, 1024)
+        turn_z(0, 0)
+        relu_z(0, 1)
         turn_h(3)
+        mul_gain(0, 1)
+        relu_z(1, 0)
+        turn_z(0, 1)
+        load_w2(3, 1, 0, 1024)
+        add_skip(0, 0)
+        il_s(5, 432, 512)
+        mm2(1, 1)
+        mul_gain(1, 0)
+        copy_h(3)
+        q_h(2)
+        mm1(4, 0)
+        add_skip(0, 1)
+        relu_z(1, 1)
         q_w(5)
         mm1(4, 1)
-        mul_gain(0, 1)
-        add_b1(4, 1)
-        mm2(1, 1)
-        relu_h(3)
-        il_s(7, 288)
-        mm1(5, 0)
-        il_s(8, 288)
-        q_h(3)
-        il_v(7, 288)
-        turn_z(0, 0)
-        il_v(8, 288)
-        add_b1(5, 0)
-        relu_z(1, 1)
-        turn_z(0, 1)
-        mm2(2, 0)
-        add_skip(0, 0)
-        q_w(8)
-        mul_gain(1, 0)
-        relu_z(2, 0)
-        turn_h(4)
-        q_w(7)
-        mm1(5, 1)
-        mul_gain(1, 1)
-        add_b1(5, 1)
-        mm2(2, 1)
-        add_skip(0, 1)
-        relu_h(4)
-        il_s(9, 288)
-        mm1(6, 0)
-        il_s(10, 288)
-        q_h(4)
-        il_v(9, 288)
-        turn_z(1, 0)
-        il_v(10, 288)
-        add_b1(6, 0)
-        relu_z(2, 1)
-        turn_z(1, 1)
-        mm2(3, 0)
         cast_y(0)
+        q_h(3)
+        turn_z(1, 0)
+        il_v(7, 480)
+        mm2(2, 0)
+        relu_h(4, 0)
+        mm2(2, 1)
+        relu_h(4, 1)
+        mul_gain(1, 1)
+        mm1(5, 0)
         add_skip(1, 0)
-        q_w(10)
-        mul_gain(2, 0)
-        relu_z(3, 0)
-        turn_h(5)
-        q_w(9)
-        mm1(6, 1)
-        mul_gain(2, 1)
-        add_b1(6, 1)
-        mm2(3, 1)
-        add_skip(1, 1)
-        relu_h(5)
-        il_s(11, 288)
-        mm1(7, 0)
-        il_s(12, 288)
-        q_h(5)
-        il_v(11, 288)
-        turn_z(2, 0)
-        il_v(12, 288)
-        add_b1(7, 0)
-        relu_z(3, 1)
+        il_s(7, 480, 512)
+        relu_z(2, 0)
+        il_v(8, 496)
+        rows_h(4)
+        relu_h(5, 0)
         turn_y(0)
-        turn_z(2, 1)
-        mm2(4, 0)
+        turn_z(1, 1)
+        relu_z(2, 1)
+        q_w(7)
+        mm2(3, 0)
+        split_h(4)
+        add_skip(1, 1)
         copy_y(0)
+        mul_gain(2, 1)
+        mm1(5, 1)
+        store_y(1)
+        load_skip(3)
+        mul_gain(2, 0)
+        il_s(8, 496, 512)
         cast_y(1)
+        turn_h(4)
+        q_w(8)
+        turn_z(2, 0)
+        il_v(11, 432)
+        mm1(6, 0)
+        il_s(10, 448, 512)
+        copy_h(4)
+        mm2(3, 1)
+        il_v(9, 480)
+        relu_h(5, 1)
+        turn_z(2, 1)
+        rows_h(5)
+        il_s(9, 480, 512)
+        relu_z(3, 0)
         add_skip(2, 0)
-        q_w(12)
-        mul_gain(3, 0)
-        relu_z(4, 0)
-        turn_h(6)
-        q_w(11)
-        mm1(7, 1)
-        mul_gain(3, 1)
-        add_b1(7, 1)
-        mm2(4, 1)
-        add_skip(2, 1)
-        relu_h(6)
-        il_s(13, 288)
-        il_s(14, 288)
-        q_h(6)
-        il_v(13, 288)
-        turn_z(3, 0)
-        il_v(14, 288)
-        relu_z(4, 1)
         turn_y(1)
-        turn_z(3, 1)
-        mm2(5, 0)
-        store_y(0)
+        mm1(6, 1)
+        relu_h(6, 0)
+        q_h(4)
+        mul_gain(3, 0)
+        relu_z(3, 1)
+        q_w(9)
+        mm1(7, 0)
         copy_y(1)
+        add_skip(2, 1)
+        turn_z(3, 0)
+        split_h(5)
+        mul_gain(3, 1)
+        store_y(2)
+        store_y(0)
+        il_v(10, 448)
+        turn_z(3, 1)
+        il_s(11, 432, 512)
+        turn_h(5)
+        relu_h(6, 1)
+        rows_h(6)
         q_y(0)
         cast_y(2)
+        il_v(12, 400)
+        store_codes(0)
+        mm1(7, 1)
+        copy_h(5)
+        q_w(10)
+        split_h(6)
+        q_h(5)
+        turn_y(2)
+        q_y(1)
+        il_s(13, 480, 512)
+        relu_h(7, 0)
+        il_v(13, 480)
+        mm2(4, 0)
+        store_codes(1)
+        copy_y(2)
+        relu_z(4, 0)
         add_skip(3, 0)
-        q_w(14)
-        mul_gain(4, 0)
-        relu_z(5, 0)
-        turn_h(7)
+        turn_h(6)
         q_w(13)
+        mm2(4, 1)
+        il_s(12, 400, 512)
+        add_skip(3, 1)
+        copy_h(6)
+        q_w(11)
+        mm2(5, 0)
+        relu_z(4, 1)
+        store_y(3)
+        mul_gain(4, 0)
+        relu_h(7, 1)
         mul_gain(4, 1)
         mm2(5, 1)
-        add_skip(3, 1)
-        relu_h(7)
-        il_s(15, 288)
-        q_h(7)
-        il_v(15, 288)
-        turn_z(4, 0)
-        relu_z(5, 1)
-        turn_y(2)
-        turn_z(4, 1)
-        mm2(6, 0)
-        store_y(1)
-        copy_y(2)
-        q_y(1)
+        q_w(12)
         cast_y(3)
-        add_skip(4, 0)
-        mul_gain(5, 0)
-        relu_z(6, 0)
-        q_w(15)
-        mul_gain(5, 1)
-        store_codes(0)
-        mm2(6, 1)
-        add_skip(4, 1)
-        turn_z(5, 0)
-        relu_z(6, 1)
+        rows_h(7)
+        il_v(14, 464)
+        turn_z(4, 1)
+        il_s(15, 480, 512)
         turn_y(3)
-        turn_z(5, 1)
-        mm2(7, 0)
-        store_y(2)
+        split_h(7)
+        turn_z(4, 0)
+        add_skip(4, 1)
         copy_y(3)
         q_y(2)
-        cast_y(4)
-        add_skip(5, 0)
-        mul_gain(6, 0)
-        relu_z(7, 0)
-        mul_gain(6, 1)
-        store_codes(1)
-        mm2(7, 1)
-        add_skip(5, 1)
-        turn_z(6, 0)
-        relu_z(7, 1)
-        turn_y(4)
-        turn_z(6, 1)
-        store_y(3)
-        copy_y(4)
-        q_y(3)
-        cast_y_v(5)
-        add_skip(6, 0)
-        mul_gain(7, 0)
-        mul_gain(7, 1)
-        store_codes(2)
-        add_skip(6, 1)
-        turn_z(7, 0)
-        turn_y(5)
-        turn_z(7, 1)
+        il_s(14, 464, 512)
+        q_h(6)
+        turn_h(7)
+        relu_z(5, 0)
+        q_w(14)
+        add_skip(4, 0)
+        copy_h(7)
+        relu_z(5, 1)
         store_y(4)
-        copy_y(5)
-        q_y(4)
-        cast_y_v(6)
-        add_skip(7, 0)
+        q_h(7)
+        mm2(6, 0)
+        il_v(15, 480)
+        cast_y(4)
+        mm2(6, 1)
+        mul_gain(5, 0)
+        relu_z(6, 0)
+        q_y(3)
+        turn_z(5, 0)
+        q_w(15)
+        mul_gain_s(5, 1)
         store_codes(3)
-        add_skip(7, 1)
-        turn_y(6)
+        turn_y(4)
+        add_skip(5, 0)
+        relu_z(6, 1)
+        turn_z(5, 1)
+        mm2(7, 0)
+        mul_gain(6, 0)
+        copy_y(4)
+        mul_gain(6, 1)
+        turn_z(6, 0)
+        add_skip(5, 1)
+        relu_z(7, 0)
+        mm2(7, 1)
+        add_skip(6, 0)
         store_y(5)
-        copy_y(6)
-        q_y(5)
-        cast_y_v(7)
+        cast_y(5)
+        turn_z(6, 1)
+        mul_gain(7, 0)
+        q_y(4)
+        turn_z(7, 0)
+        add_skip(6, 1)
+        relu_z(7, 1)
         store_codes(4)
-        turn_y(7)
+        turn_y(5)
+        add_skip(7, 0)
         store_y(6)
-        copy_y(7)
-        q_y(6)
-        store_codes(5)
+        copy_y(5)
+        store_codes(2)
+        mul_gain(7, 1)
+        cast_y_v(6)
+        turn_z(7, 1)
+        q_y(5)
+        turn_y(6)
+        add_skip(7, 1)
         store_scales(0, 768)
+        store_codes(5)
+        copy_y(6)
         store_y(7)
-        q_y(7)
+        cast_y_v(7)
+        q_y(6)
+        turn_y(7)
         store_codes(6)
+        copy_y(7)
+        q_y(7)
         store_codes(7)
         store_scales(768, 1024)

@@ -19,11 +19,14 @@ P = 128
 HALF = 512
 UNITS = 2 * NETS
 VCOLS = 288
-NGRP = 3
-NWQ = 8
+NGRP = 4
+NWQ = 7
 NY = 6
-NRAW = 6
+NRAW = 5
 NHQ = 4
+NB = 3
+NBANK = 8
+NZ = 3
 FAST = True
 WA = 3
 
@@ -47,33 +50,35 @@ def tile_mask_hypernetwork_trunk_h2_kernel(
         (ident_bf,) = tiles("ident_bf", 1, [P, P], BF16)
         (vec_bf,) = tiles("vec_bf", 1, [96, P], BF16)
         (vec_rows,) = tiles("vec_rows", 1, [P, P], F32)
-        (vec_cols,) = tiles("vec_cols", 1, [P, 96], F32)
+        (b1_cols,) = tiles("b1_cols", 1, [P, 32], F32)
+        (out_cols,) = tiles("out_cols", 1, [P, 64], F32)
         (x_codes,) = tiles("x_codes", 1, [P, 2, NETS * TOK], U32)
         (x_sc,) = tiles("x_sc", 1, [P, 2, NETS * TOK], U8)
-        w1_codes = tiles("w1_codes", NETS, [P, 2, 2 * F], U8)
+        (w1_codes,) = tiles("w1_codes", 1, [P, 2, 2 * NETS * F], U8)
         (w1_sc,) = tiles("w1_sc", 1, [P, 2, NETS * F], U8)
         w2_raw = tiles("w2_raw", NRAW, [P, 4, D], BF16)
         skip_sb = tiles("skip_sb", NETS, [P, 2, D], BF16)
         w2_grp = tiles("w2_grp", NGRP, [P, HALF, 4], BF16)
         w2_codes = tiles("w2_codes", NWQ, [P, 2, HALF], U32)
         w2_sc = tiles("w2_sc", NWQ, [P, 2, HALF], U8)
-        h_rows = tiles("h_rows", 2, [P, 2, 2, 2 * P], BF16)
-        h_cols = tiles("h_cols", 2, [P, 4, TOK], BF16)
-        h_grp = tiles("h_grp", 2, [P, 2 * TOK], F32)
+        h_rows = tiles("h_rows", NB, [P, 2, 2, 2 * P], BF16)
+        h_cols = tiles("h_cols", NB, [P, 4, TOK], BF16)
+        h_grp = tiles("h_grp", NB, [P, 2 * TOK], F32)
         h_codes = tiles("h_codes", NHQ, [P, 2, TOK], U32)
         h_sc = tiles("h_sc", NHQ, [P, 2, TOK], U8)
-        z_cols = tiles("z_cols", 2, [P, 4, TOK], F32)
+        z_cols = tiles("z_cols", NZ, [P, 4, TOK], F32)
         y_rows = tiles("y_rows", NY, [P, 2, HALF], F32)
-        y_bf = tiles("y_bf", 2, [P, 2, 2, 2 * P], BF16)
-        y_grp = tiles("y_grp", 2, [P, 2 * TOK], F32)
+        y_bf = tiles("y_bf", NB, [P, 2, 2, 2 * P], BF16)
+        y_grp = tiles("y_grp", NB, [P, 2 * TOK], F32)
         (y_codes,) = tiles("y_codes", 1, [P, 2, NETS * TOK], U32)
         (y_sc,) = tiles("y_sc", 1, [P, 2, NETS * TOK], U8)
 
-        h_bank = banks("h_bank", 2)
-        (ht_bank,) = banks("ht_bank", 1)
-        z_bank = banks("z_bank", 2)
-        zt_bank = banks("zt_bank", 2)
-        (word_bank,) = banks("word_bank", 1)
+        psum = banks("bank", NBANK)
+        bank_of = {}
+
+        def take_bank(*key):
+            bank_of[key] = psum[len(bank_of) % NBANK]
+            return bank_of[key]
 
         def load_w2(i, g, c0, c1):
             rows = w2[i, g * HALF : (g + 1) * HALF, :].rearrange("(p j) d -> p j d", j=4)
@@ -91,11 +96,10 @@ def tile_mask_hypernetwork_trunk_h2_kernel(
             words = x_words.rearrange("g p n t -> p g (n t)")
             nc.sync.dma_start(out=x_codes[:, :, c0:c1].bitcast(I32), in_=words[:, :, 4 * c0 : 4 * c1].bitcast(I32))
 
-        def load_w1(i):
+        def load_w1(i0, i1):
             words = w1_words.rearrange("g p n -> p g n")
-            nc.sync.dma_start(
-                out=w1_codes[i][:].bitcast(I32), in_=words[:, :, 2 * F * i : 2 * F * (i + 1)].bitcast(I32)
-            )
+            cols = slice(2 * F * i0, 2 * F * i1)
+            nc.sync.dma_start(out=w1_codes[:, :, cols].bitcast(I32), in_=words[:, :, cols].bitcast(I32))
 
         def load_skip(i):
             nc.sync.dma_start(out=skip_sb[i][:], in_=skip[i].rearrange("(tt p) d -> p tt d", p=P))
@@ -110,19 +114,21 @@ def tile_mask_hypernetwork_trunk_h2_kernel(
         def vec_zero():
             nc.vector.memset(vec_rows[:], 0.0)
 
-        def vec_load():
-            nc.scalar.dma_start(out=vec_bf[0:32, :], in_=b2.rearrange("t (c n) -> (t c) n", n=P))
-            nc.scalar.dma_start(out=vec_bf[32:64, :], in_=gain.rearrange("t (c n) -> (t c) n", n=P))
-            nc.scalar.dma_start(out=vec_bf[64:96, :], in_=b1.rearrange("t (c n) -> (t c) n", n=P))
+        def vec_load(n):
+            src = (b1, b2, gain)[n]
+            nc.sync.dma_start(out=vec_bf[32 * n : 32 * n + 32, :], in_=src.rearrange("t (c n) -> (t c) n", n=P))
 
-        def vec_cast():
-            nc.scalar.activation(out=vec_rows[0:96, :], in_=vec_bf[:], func=ACT.Identity)
+        def vec_cast(s):
+            for n in ((0,), (1, 2))[s]:
+                rows = slice(32 * n, 32 * n + 32)
+                nc.scalar.activation(out=vec_rows[rows, :], in_=vec_bf[rows, :], func=ACT.Identity)
 
-        def vec_turn():
-            nc.tensor.transpose(word_bank[:, 0:P], vec_rows[:], ident[:])
+        def vec_turn(s):
+            nc.tensor.transpose(take_bank("vec", s)[:, 0:P], vec_rows[:], ident[:])
 
-        def vec_copy():
-            nc.scalar.copy(out=vec_cols[:], in_=word_bank[:, 0:96])
+        def vec_copy(s):
+            cols = (slice(0, 32), slice(32, 96))[s]
+            nc.scalar.copy(out=(b1_cols, out_cols)[s][:], in_=bank_of[("vec", s)][:, cols])
 
         def il_views(k, c0, c1):
             unit, g = divmod(k, 2)
@@ -160,6 +166,7 @@ def tile_mask_hypernetwork_trunk_h2_kernel(
         def mm1(q, s):
             if 0 <= q < UNITS:
                 i, fh = divmod(q, 2)
+                bank = take_bank("h", q, s)
                 for fl in range(2):
                     f0 = fh * HALF + (2 * s + fl) * P
                     for tt in range(2):
@@ -167,8 +174,8 @@ def tile_mask_hypernetwork_trunk_h2_kernel(
                         c0 = fl * TOK + tt * P
                         for g in range(2):
                             nc.tensor.matmul_mx(
-                                out=h_bank[s][:, c0 : c0 + P],
-                                lhsT=w1_codes[i][:, g, 2 * f0 : 2 * (f0 + P)].bitcast(FP4X4),
+                                out=bank[:, c0 : c0 + P],
+                                lhsT=w1_codes[:, g, 2 * (i * F + f0) : 2 * (i * F + f0 + P)].bitcast(FP4X4),
                                 lhsT_scale=w1_sc[:, g, i * F + f0 : i * F + f0 + P],
                                 rhs=x_codes[:, g, t0 : t0 + P].bitcast(FP8X4),
                                 rhs_scale=x_sc[:, g, t0 : t0 + P],
@@ -179,30 +186,31 @@ def tile_mask_hypernetwork_trunk_h2_kernel(
         def relu_h(q, s):
             if 0 <= q < UNITS:
                 for fl in range(2):
-                    c = 64 + 4 * q + 2 * s + fl
+                    c = 4 * q + 2 * s + fl
                     nc.scalar.activation(
-                        out=h_cols[q % 2][:, 2 * s + fl, :],
-                        in_=h_bank[s][:, fl * TOK : (fl + 1) * TOK],
+                        out=h_cols[q % NB][:, 2 * s + fl, :],
+                        in_=bank_of[("h", q, s)][:, fl * TOK : (fl + 1) * TOK],
                         func=ACT.Relu,
-                        bias=vec_cols[:, c : c + 1],
+                        bias=b1_cols[:, c : c + 1],
                     )
 
         def rows_h(q):
             if 0 <= q < UNITS:
+                bank = take_bank("rows", q)
                 for tt in range(2):
                     for fl in range(4):
                         c0 = tt * HALF + fl * P
                         nc.tensor.transpose(
-                            ht_bank[:].bitcast(BF16)[:, c0 : c0 + P],
-                            h_cols[q % 2][:, fl, tt * P : (tt + 1) * P],
+                            bank[:].bitcast(BF16)[:, c0 : c0 + P],
+                            h_cols[q % NB][:, fl, tt * P : (tt + 1) * P],
                             ident_bf[:],
                         )
 
         def split_h(q):
             if 0 <= q < UNITS:
                 nc.scalar.copy(
-                    out=h_rows[q % 2][:].rearrange("p u tt w -> p u (tt w)").bitcast(F32),
-                    in_=ht_bank[:].rearrange("p (w u) -> p u w", u=2),
+                    out=h_rows[q % NB][:].rearrange("p u tt w -> p u (tt w)").bitcast(F32),
+                    in_=bank_of[("rows", q)][:].rearrange("p (w u) -> p u w", u=2),
                 )
 
         def turn_words(bank, rows):
@@ -213,36 +221,37 @@ def tile_mask_hypernetwork_trunk_h2_kernel(
 
         def split_h_v(q):
             nc.vector.tensor_copy(
-                out=h_rows[q % 2][:].rearrange("p u tt w -> p u (tt w)").bitcast(F32),
-                in_=ht_bank[:].rearrange("p (w u) -> p u w", u=2),
+                out=h_rows[q % NB][:].rearrange("p u tt w -> p u (tt w)").bitcast(F32),
+                in_=bank_of[("rows", q)][:].rearrange("p (w u) -> p u w", u=2),
             )
 
         def turn_h(q):
             if 0 <= q < UNITS:
-                turn_words(word_bank, h_rows[q % 2])
+                turn_words(take_bank("hw", q), h_rows[q % NB])
 
         def copy_h(q):
             if 0 <= q < UNITS:
                 nc.scalar.copy(
-                    out=h_grp[q % 2][:].rearrange("p (r u) -> p r u", u=2),
-                    in_=word_bank[:].rearrange("p (u r) -> p r u", u=2),
+                    out=h_grp[q % NB][:].rearrange("p (r u) -> p r u", u=2),
+                    in_=bank_of[("hw", q)][:].rearrange("p (u r) -> p r u", u=2),
                 )
 
         def q_h(q):
             if 0 <= q < UNITS:
                 i, fh = divmod(q, 2)
                 nc.vector.quantize_mx(
-                    out=h_codes[i % NHQ][:, fh, :].bitcast(FP8X4), scales=h_sc[i % NHQ][:, fh, :], in_=h_grp[q % 2][:].bitcast(BF16)
+                    out=h_codes[i % NHQ][:, fh, :].bitcast(FP8X4), scales=h_sc[i % NHQ][:, fh, :], in_=h_grp[q % NB][:].bitcast(BF16)
                 )
 
         def mm2(p, z):
             if 0 <= p < UNITS:
                 i = p // 2
+                bank = take_bank("z", p, z)
                 for dl in range(2):
                     d0 = (2 * z + dl) * P
                     for g in range(2):
                         nc.tensor.matmul_mx(
-                            out=z_bank[z][:, dl * TOK : (dl + 1) * TOK],
+                            out=bank[:, dl * TOK : (dl + 1) * TOK],
                             lhsT=w2_codes[p % NWQ][:, g, d0 : d0 + P].bitcast(FP8X4),
                             lhsT_scale=w2_sc[p % NWQ][:, g, d0 : d0 + P],
                             rhs=h_codes[i % NHQ][:, g, :].bitcast(FP8X4),
@@ -256,34 +265,35 @@ def tile_mask_hypernetwork_trunk_h2_kernel(
                 for dl in range(2):
                     c = 4 * p + 2 * z + dl
                     nc.scalar.activation(
-                        out=z_cols[p % 2][:, 2 * z + dl, :],
-                        in_=z_bank[z][:, dl * TOK : (dl + 1) * TOK],
+                        out=z_cols[p % NZ][:, 2 * z + dl, :],
+                        in_=bank_of[("z", p, z)][:, dl * TOK : (dl + 1) * TOK],
                         func=ACT.Relu,
-                        bias=vec_cols[:, c : c + 1],
+                        bias=out_cols[:, c : c + 1],
                     )
 
         def mul_gain(p, z):
             if 0 <= p < UNITS:
                 for dl in range(2):
                     c = 32 + 4 * p + 2 * z + dl
-                    zc = z_cols[p % 2][:, 2 * z + dl, :]
+                    zc = z_cols[p % NZ][:, 2 * z + dl, :]
                     nc.vector.tensor_scalar(
-                        out=zc, in0=zc, scalar1=vec_cols[:, c : c + 1], scalar2=None, op0=ALU.mult
+                        out=zc, in0=zc, scalar1=out_cols[:, c : c + 1], scalar2=None, op0=ALU.mult
                     )
 
         def mul_gain_s(p, z):
             for dl in range(2):
                 c = 32 + 4 * p + 2 * z + dl
-                zc = z_cols[p % 2][:, 2 * z + dl, :]
-                nc.scalar.activation(out=zc, in_=zc, func=ACT.Copy, scale=vec_cols[:, c : c + 1])
+                zc = z_cols[p % NZ][:, 2 * z + dl, :]
+                nc.scalar.activation(out=zc, in_=zc, func=ACT.Copy, scale=out_cols[:, c : c + 1])
 
         def turn_z(p, z):
             if 0 <= p < UNITS:
+                bank = take_bank("zt", p, z)
                 for tt in range(2):
                     for dl in range(2):
                         c0 = tt * TOK + dl * P
                         nc.tensor.transpose(
-                            zt_bank[z][:, c0 : c0 + P], z_cols[p % 2][:, 2 * z + dl, tt * P : (tt + 1) * P], ident[:]
+                            bank[:, c0 : c0 + P], z_cols[p % NZ][:, 2 * z + dl, tt * P : (tt + 1) * P], ident[:]
                         )
 
         def add_skip(p, z):
@@ -292,8 +302,19 @@ def tile_mask_hypernetwork_trunk_h2_kernel(
                 d0 = h * HALF + z * 256
                 nc.vector.tensor_tensor(
                     out=y_rows[p % NY][:, :, z * 256 : (z + 1) * 256],
-                    in0=zt_bank[z][:].rearrange("p (tt d) -> p tt d", tt=2),
+                    in0=bank_of[("zt", p, z)][:].rearrange("p (tt d) -> p tt d", tt=2),
                     in1=skip_sb[i][:, :, d0 : d0 + 256],
+                    op=ALU.add,
+                )
+
+        def add_skip_bf(p, z):
+            i, h = divmod(p, 2)
+            d0 = h * HALF + z * 256
+            for tt in range(2):
+                nc.vector.tensor_tensor(
+                    out=y_bf[p % NB][:, :, tt, z * P : (z + 1) * P].rearrange("p u (w e) -> p u w e", e=2),
+                    in0=bank_of[("zt", p, z)][:, tt * TOK : (tt + 1) * TOK].rearrange("p (w u e) -> p u w e", u=2, e=2),
+                    in1=skip_sb[i][:, tt, d0 : d0 + 256].rearrange("p (w u e) -> p u w e", u=2, e=2),
                     op=ALU.add,
                 )
 
@@ -303,8 +324,14 @@ def tile_mask_hypernetwork_trunk_h2_kernel(
                 dst = out_0[i].rearrange("(tt p) d -> p tt d", p=P)[:, :, h * HALF : (h + 1) * HALF]
                 nc.sync.dma_start(out=dst, in_=y_rows[p % NY][:])
 
+        def store_y_half(p, z):
+            i, h = divmod(p, 2)
+            d0 = h * HALF + z * 256
+            dst = out_0[i].rearrange("(tt p) d -> p tt d", p=P)[:, :, d0 : d0 + 256]
+            nc.sync.dma_start(out=dst, in_=y_rows[p % NY][:, :, z * 256 : (z + 1) * 256])
+
         def cast_views(p):
-            dst = y_bf[p % 2][:].rearrange("p u tt (w e) -> p u (tt w) e", e=2)
+            dst = y_bf[p % NB][:].rearrange("p u tt (w e) -> p u (tt w) e", e=2)
             return dst, y_rows[p % NY][:].rearrange("p tt (w u e) -> p u (tt w) e", u=2, e=2)
 
         def cast_y(p):
@@ -319,13 +346,13 @@ def tile_mask_hypernetwork_trunk_h2_kernel(
 
         def turn_y(p):
             if 0 <= p < UNITS:
-                turn_words(word_bank, y_bf[p % 2])
+                turn_words(take_bank("yw", p), y_bf[p % NB])
 
         def copy_y(p):
             if 0 <= p < UNITS:
                 nc.scalar.copy(
-                    out=y_grp[p % 2][:].rearrange("p (r u) -> p r u", u=2),
-                    in_=word_bank[:].rearrange("p (u r) -> p r u", u=2),
+                    out=y_grp[p % NB][:].rearrange("p (r u) -> p r u", u=2),
+                    in_=bank_of[("yw", p)][:].rearrange("p (u r) -> p r u", u=2),
                 )
 
         def q_y(p):
@@ -333,7 +360,7 @@ def tile_mask_hypernetwork_trunk_h2_kernel(
                 i, h = divmod(p, 2)
                 cols = slice(i * TOK, (i + 1) * TOK)
                 nc.vector.quantize_mx(
-                    out=y_codes[:, h, cols].bitcast(FP8X4), scales=y_sc[:, h, cols], in_=y_grp[p % 2][:].bitcast(BF16)
+                    out=y_codes[:, h, cols].bitcast(FP8X4), scales=y_sc[:, h, cols], in_=y_grp[p % NB][:].bitcast(BF16)
                 )
 
         def store_codes(p):
@@ -344,294 +371,302 @@ def tile_mask_hypernetwork_trunk_h2_kernel(
 
         def store_scales(c0, c1):
             rows = out_2.rearrange("g q m -> q g m")
+            queue = nc.sync if c0 == 0 else nc.scalar
             for quad in range(4):
-                nc.sync.dma_start(
+                queue.dma_start(
                     out=rows[4 * quad : 4 * quad + 4, :, c0:c1].bitcast(I32),
                     in_=y_sc[32 * quad : 32 * quad + 4, :, c0:c1].bitcast(I32),
                 )
 
         identity()
-        vec_load()
+        vec_zero()
+        load_x(0, 256)
         zero(w1_sc, 0, 1024)
-        load_w1(0)
+        vec_load(0)
+        zero(x_sc, 0, 1024)
         zero(w1_sc, 1024, 4096)
         load_scales(w1_sc, w1_scales, 0, 1024)
-        vec_zero()
-        zero(x_sc, 0, 1024)
-        load_w2(0, 0, 0, 512)
-        load_x(0, 256)
+        load_w1(0, 1)
         load_scales(x_sc, x_scales, 0, 256)
-        vec_cast()
-        vec_turn()
+        vec_cast(0)
+        load_w2(0, 0, 0, 512)
+        vec_load(1)
         load_w2(0, 1, 0, 512)
-        load_w2(0, 1, 512, 1024)
-        vec_copy()
-        load_scales(w1_sc, w1_scales, 1024, 2048)
-        il_v(0, 320)
-        il_s(0, 320, 512)
-        load_w2(0, 0, 512, 1024)
-        mm1(0, 0)
+        vec_turn(0)
+        vec_copy(0)
         load_scales(x_sc, x_scales, 256, 1024)
-        q_w(0)
-        il_v(1, 496)
+        vec_load(2)
+        mm1(0, 0)
+        load_w2(0, 1, 512, 1024)
+        load_w2(0, 0, 512, 1024)
         mm1(0, 1)
+        il_v(0, 480)
         relu_h(0, 0)
-        il_v(3, 384)
+        load_scales(w1_sc, w1_scales, 1024, 2048)
+        il_s(0, 480, 512)
         mm1(1, 0)
+        il_v(1, 496)
+        load_w1(1, 2)
         load_x(256, 512)
-        load_w1(1)
         relu_h(0, 1)
-        load_w2(1, 0, 0, 1024)
-        rows_h(0)
-        il_s(1, 496, 512)
-        il_s(3, 384, 512)
-        q_w(1)
         mm1(1, 1)
-        load_scales(w1_sc, w1_scales, 2048, 4096)
+        q_w(0)
         relu_h(1, 0)
-        split_h_v(0)
-        load_w2(1, 1, 0, 1024)
-        il_v(2, 480)
+        rows_h(0)
+        load_w2(1, 0, 0, 1024)
         relu_h(1, 1)
-        turn_h(0)
-        load_w1(2)
         rows_h(1)
-        il_s(2, 480, 512)
-        copy_h(0)
-        q_w(3)
+        split_h_v(0)
+        vec_cast(1)
+        load_w2(1, 1, 0, 1024)
+        il_s(3, 448, 512)
         load_skip(0)
-        split_h_v(1)
-        mm1(2, 0)
-        q_w(2)
-        q_h(0)
-        mm1(2, 1)
-        relu_h(2, 0)
+        il_v(3, 448)
+        load_scales(w1_sc, w1_scales, 2048, 4096)
+        vec_turn(1)
+        turn_h(0)
+        split_h(1)
+        il_v(2, 432)
+        il_s(1, 496, 512)
+        copy_h(0)
         turn_h(1)
+        vec_copy(1)
+        q_h(0)
         load_x(512, 1024)
-        il_v(4, 496)
-        relu_h(2, 1)
-        load_w2(2, 0, 0, 1024)
-        mm1(3, 0)
-        load_w1(3)
         copy_h(1)
-        load_skip(1)
-        rows_h(2)
-        relu_h(3, 0)
-        load_w2(2, 1, 0, 1024)
+        q_w(1)
+        il_s(2, 432, 512)
         q_h(1)
-        mm1(3, 1)
-        il_v(6, 496)
-        il_s(4, 496, 512)
-        split_h(2)
         mm2(0, 0)
-        relu_h(3, 1)
-        turn_h(2)
-        q_w(4)
-        il_s(6, 496, 512)
-        rows_h(3)
+        q_w(3)
+        q_w(2)
+        load_w1(2, 3)
+        mm1(2, 0)
+        il_v(4, 400)
         relu_z(0, 0)
-        q_w(6)
-        load_skip(2)
-        mm2(0, 1)
-        copy_h(2)
+        mm1(2, 1)
+        il_v(6, 400)
+        relu_h(2, 0)
+        mm1(3, 1)
+        load_w2(2, 0, 0, 1024)
+        relu_h(2, 1)
         mul_gain(0, 0)
-        mm2(1, 0)
-        il_v(5, 432)
-        split_h(3)
-        load_w2(3, 0, 0, 1024)
+        mm1(3, 0)
+        il_s(4, 400, 512)
+        rows_h(2)
+        load_w2(2, 1, 0, 1024)
+        relu_h(3, 1)
+        load_w1(3, 4)
         turn_z(0, 0)
-        relu_z(0, 1)
-        turn_h(3)
-        mul_gain(0, 1)
-        relu_z(1, 0)
-        turn_z(0, 1)
-        load_w2(3, 1, 0, 1024)
+        q_w(4)
+        load_skip(1)
+        mm2(0, 1)
+        relu_h(3, 0)
+        split_h_v(2)
+        il_s(5, 416, 512)
+        rows_h(3)
         add_skip(0, 0)
-        il_s(5, 432, 512)
+        relu_z(0, 1)
+        il_v(5, 416)
+        turn_h(2)
+        mm2(1, 0)
+        split_h(3)
         mm2(1, 1)
-        mul_gain(1, 0)
-        copy_h(3)
-        q_h(2)
-        mm1(4, 0)
-        add_skip(0, 1)
-        relu_z(1, 1)
-        q_w(5)
-        mm1(4, 1)
-        cast_y(0)
-        q_h(3)
-        turn_z(1, 0)
+        copy_h(2)
+        mul_gain(0, 1)
         il_v(7, 480)
-        mm2(2, 0)
-        relu_h(4, 0)
-        mm2(2, 1)
-        relu_h(4, 1)
-        mul_gain(1, 1)
-        mm1(5, 0)
-        add_skip(1, 0)
+        turn_h(3)
+        il_s(6, 400, 512)
+        turn_z(0, 1)
+        relu_z(1, 0)
+        mm1(4, 1)
+        load_w2(3, 1, 0, 1024)
+        q_w(6)
+        load_w2(3, 0, 0, 1024)
+        relu_z(1, 1)
+        mm1(4, 0)
+        mul_gain(1, 0)
         il_s(7, 480, 512)
-        relu_z(2, 0)
-        il_v(8, 496)
+        q_h(2)
+        copy_h(3)
+        turn_z(1, 0)
+        mul_gain(1, 1)
+        add_skip(0, 1)
+        relu_h(4, 1)
+        turn_z(1, 1)
+        q_w(5)
+        mm1(5, 0)
+        relu_h(4, 0)
+        q_h(3)
+        il_s(10, 480, 512)
+        mm2(2, 0)
+        il_v(8, 464)
+        cast_y(0)
         rows_h(4)
+        il_v(10, 480)
         relu_h(5, 0)
         turn_y(0)
-        turn_z(1, 1)
-        relu_z(2, 1)
-        q_w(7)
-        mm2(3, 0)
-        split_h(4)
-        add_skip(1, 1)
-        copy_y(0)
-        mul_gain(2, 1)
+        relu_z(2, 0)
         mm1(5, 1)
-        store_y(1)
-        load_skip(3)
+        add_skip(1, 0)
+        split_h(4)
+        mm2(2, 1)
         mul_gain(2, 0)
-        il_s(8, 496, 512)
-        cast_y(1)
-        turn_h(4)
-        q_w(8)
+        copy_y(0)
+        add_skip(1, 1)
         turn_z(2, 0)
-        il_v(11, 432)
-        mm1(6, 0)
-        il_s(10, 448, 512)
-        copy_h(4)
-        mm2(3, 1)
-        il_v(9, 480)
         relu_h(5, 1)
-        turn_z(2, 1)
+        q_w(7)
+        store_y(1)
+        turn_h(4)
+        il_s(8, 464, 512)
+        il_v(9, 480)
         rows_h(5)
-        il_s(9, 480, 512)
-        relu_z(3, 0)
+        cast_y(1)
+        mm2(3, 0)
+        copy_h(4)
         add_skip(2, 0)
-        turn_y(1)
-        mm1(6, 1)
-        relu_h(6, 0)
-        q_h(4)
-        mul_gain(3, 0)
-        relu_z(3, 1)
-        q_w(9)
-        mm1(7, 0)
-        copy_y(1)
-        add_skip(2, 1)
-        turn_z(3, 0)
-        split_h(5)
-        mul_gain(3, 1)
-        store_y(2)
-        store_y(0)
-        il_v(10, 448)
-        turn_z(3, 1)
-        il_s(11, 432, 512)
-        turn_h(5)
-        relu_h(6, 1)
-        rows_h(6)
+        mm1(6, 0)
+        relu_z(2, 1)
         q_y(0)
-        cast_y(2)
-        il_v(12, 400)
+        mm1(7, 0)
+        il_v(11, 480)
+        il_s(11, 480, 512)
         store_codes(0)
-        mm1(7, 1)
-        copy_h(5)
-        q_w(10)
-        split_h(6)
-        q_h(5)
-        turn_y(2)
-        q_y(1)
-        il_s(13, 480, 512)
+        store_y(0)
+        mm1(6, 1)
+        il_s(9, 480, 512)
+        load_skip(2)
+        split_h(5)
+        mul_gain(2, 1)
+        relu_z(3, 0)
+        q_w(9)
+        turn_z(2, 1)
+        relu_h(6, 0)
+        q_w(11)
+        turn_h(5)
+        mm2(3, 1)
         relu_h(7, 0)
-        il_v(13, 480)
+        mul_gain(3, 0)
+        q_w(8)
+        turn_y(1)
+        relu_h(6, 1)
+        mm1(7, 1)
+        q_h(4)
+        copy_h(5)
+        il_v(13, 464)
+        rows_h(6)
+        relu_z(3, 1)
+        turn_z(3, 0)
+        q_h(5)
+        copy_y(1)
+        mm2(4, 1)
+        add_skip(2, 1)
+        relu_h(7, 1)
+        mul_gain(3, 1)
+        il_v(12, 432)
+        store_y(2)
+        split_h(6)
+        turn_z(3, 1)
+        cast_y(2)
+        rows_h(7)
+        q_y(1)
         mm2(4, 0)
+        add_skip(3, 1)
+        il_s(13, 464, 512)
+        turn_h(6)
+        relu_z(4, 1)
+        q_w(10)
+        turn_y(2)
+        add_skip(3, 0)
+        relu_z(4, 0)
+        mm2(5, 1)
+        il_v(15, 464)
+        il_s(12, 432, 512)
+        store_y(3)
+        mm2(5, 0)
+        load_skip(3)
+        split_h(7)
         store_codes(1)
         copy_y(2)
-        relu_z(4, 0)
-        add_skip(3, 0)
-        turn_h(6)
-        q_w(13)
-        mm2(4, 1)
-        il_s(12, 400, 512)
-        add_skip(3, 1)
-        copy_h(6)
-        q_w(11)
-        mm2(5, 0)
-        relu_z(4, 1)
-        store_y(3)
-        mul_gain(4, 0)
-        relu_h(7, 1)
         mul_gain(4, 1)
-        mm2(5, 1)
-        q_w(12)
-        cast_y(3)
-        rows_h(7)
-        il_v(14, 464)
+        mul_gain(4, 0)
+        copy_h(6)
         turn_z(4, 1)
-        il_s(15, 480, 512)
-        turn_y(3)
-        split_h(7)
+        il_v(14, 432)
+        turn_h(7)
+        cast_y(3)
         turn_z(4, 0)
+        q_h(6)
+        q_w(13)
+        copy_h(7)
+        turn_y(3)
+        il_s(15, 464, 512)
+        q_w(12)
+        relu_z(5, 1)
+        add_skip(4, 0)
+        relu_z(5, 0)
+        q_h(7)
+        mm2(6, 1)
+        mul_gain(5, 1)
+        il_s(14, 432, 512)
         add_skip(4, 1)
         copy_y(3)
-        q_y(2)
-        il_s(14, 464, 512)
-        q_h(6)
-        turn_h(7)
-        relu_z(5, 0)
-        q_w(14)
-        add_skip(4, 0)
-        copy_h(7)
-        relu_z(5, 1)
-        store_y(4)
-        q_h(7)
-        mm2(6, 0)
-        il_v(15, 480)
-        cast_y(4)
-        mm2(6, 1)
         mul_gain(5, 0)
+        mm2(6, 0)
+        q_w(14)
+        store_y(4)
+        cast_y(4)
+        turn_z(5, 1)
+        q_w(15)
+        turn_z(5, 0)
         relu_z(6, 0)
         q_y(3)
-        turn_z(5, 0)
-        q_w(15)
-        mul_gain_s(5, 1)
-        store_codes(3)
         turn_y(4)
-        add_skip(5, 0)
-        relu_z(6, 1)
-        turn_z(5, 1)
-        mm2(7, 0)
-        mul_gain(6, 0)
-        copy_y(4)
-        mul_gain(6, 1)
-        turn_z(6, 0)
         add_skip(5, 1)
-        relu_z(7, 0)
+        relu_z(6, 1)
+        mm2(7, 0)
+        add_skip(5, 0)
         mm2(7, 1)
-        add_skip(6, 0)
+        copy_y(4)
+        mul_gain(6, 0)
+        cast_y_v(5)
         store_y(5)
-        cast_y(5)
-        turn_z(6, 1)
-        mul_gain(7, 0)
+        mul_gain_s(6, 1)
+        turn_z(6, 0)
+        q_y(2)
+        relu_z(7, 0)
         q_y(4)
-        turn_z(7, 0)
-        add_skip(6, 1)
+        turn_y(5)
+        add_skip(6, 0)
+        turn_z(6, 1)
         relu_z(7, 1)
         store_codes(4)
-        turn_y(5)
-        add_skip(7, 0)
-        store_y(6)
-        copy_y(5)
         store_codes(2)
+        mul_gain(7, 0)
+        store_codes(3)
+        add_skip(6, 1)
+        turn_z(7, 0)
         mul_gain(7, 1)
-        cast_y_v(6)
+        store_y(6)
+        cast_y(6)
+        add_skip(7, 0)
         turn_z(7, 1)
-        q_y(5)
+        add_skip_bf(7, 0)
+        store_y_half(7, 0)
+        copy_y(5)
+        add_skip_bf(7, 1)
         turn_y(6)
-        add_skip(7, 1)
-        store_scales(0, 768)
-        store_codes(5)
-        copy_y(6)
-        store_y(7)
-        cast_y_v(7)
-        q_y(6)
+        q_y(5)
         turn_y(7)
-        store_codes(6)
+        add_skip(7, 1)
+        copy_y(6)
+        store_scales(0, 768)
         copy_y(7)
+        store_codes(5)
+        store_y_half(7, 1)
+        q_y(6)
         q_y(7)
+        store_codes(6)
         store_codes(7)
         store_scales(768, 1024)

@@ -20,9 +20,9 @@ HALF = 512
 UNITS = 2 * NETS
 VCOLS = 288
 NGRP = 4
-NWQ = 7
-NY = 6
-NRAW = 5
+NWQ = 6
+NY = 5
+NRAW = 4
 NHQ = 4
 NB = 3
 NBANK = 8
@@ -52,11 +52,29 @@ def tile_mask_hypernetwork_trunk_h2_kernel(
         (vec_rows,) = tiles("vec_rows", 1, [P, P], F32)
         (b1_cols,) = tiles("b1_cols", 1, [P, 32], F32)
         (out_cols,) = tiles("out_cols", 1, [P, 64], F32)
-        (x_codes,) = tiles("x_codes", 1, [P, 2, NETS * TOK], U32)
-        (x_sc,) = tiles("x_sc", 1, [P, 2, NETS * TOK], U8)
-        (w1_codes,) = tiles("w1_codes", 1, [P, 2, 2 * NETS * F], U8)
-        (w1_sc,) = tiles("w1_sc", 1, [P, 2, NETS * F], U8)
+        def pieces(name, cuts, dtype):
+            return [
+                (c0, c1, sb.tile([P, 2, c1 - c0], dtype, name="%s%d" % (name, c0), align_bytes=64))
+                for c0, c1 in zip(cuts, cuts[1:])
+            ]
+
+        def window(parts, c0, c1):
+            ((a, tile),) = [(a, tile) for a, b, tile in parts if a <= c0 and c1 <= b]
+            return tile[:, :, c0 - a : c1 - a]
+
+        x_codes = pieces("x_codes", (0, 256, 512, 1024), U32)
+        x_sc = pieces("x_sc", (0, 256, 1024), U8)
+        w1_codes = pieces("w1_codes", (0, 2048, 4096, 6144, 8192), U8)
+        w1_sc = pieces("w1_sc", (0, 1024, 2048, 4096), U8)
+        w2_first = tiles("w2_first", 4, [P, 4, HALF], BF16)
         w2_raw = tiles("w2_raw", NRAW, [P, 4, D], BF16)
+
+        def raw_w2(i, g, c0, c1):
+            if i == 0:
+                h = c0 // HALF
+                return w2_first[2 * h + g][:, :, c0 - h * HALF : c1 - h * HALF]
+            return w2_raw[(2 * i + g - 2) % NRAW][:, :, c0:c1]
+
         skip_sb = tiles("skip_sb", NETS, [P, 2, D], BF16)
         w2_grp = tiles("w2_grp", NGRP, [P, HALF, 4], BF16)
         w2_codes = tiles("w2_codes", NWQ, [P, 2, HALF], U32)
@@ -71,7 +89,7 @@ def tile_mask_hypernetwork_trunk_h2_kernel(
         y_bf = tiles("y_bf", NB, [P, 2, 2, 2 * P], BF16)
         y_grp = tiles("y_grp", NB, [P, 2 * TOK], F32)
         (y_codes,) = tiles("y_codes", 1, [P, 2, NETS * TOK], U32)
-        (y_sc,) = tiles("y_sc", 1, [P, 2, NETS * TOK], U8)
+        y_sc = pieces("y_sc", (0, 768, 1024), U8)
 
         psum = banks("bank", NBANK)
         bank_of = {}
@@ -82,30 +100,32 @@ def tile_mask_hypernetwork_trunk_h2_kernel(
 
         def load_w2(i, g, c0, c1):
             rows = w2[i, g * HALF : (g + 1) * HALF, :].rearrange("(p j) d -> p j d", j=4)
-            nc.sync.dma_start(out=w2_raw[(2 * i + g) % NRAW][:, :, c0:c1], in_=rows[:, :, c0:c1])
+            nc.sync.dma_start(out=raw_w2(i, g, c0, c1), in_=rows[:, :, c0:c1])
 
         def load_scales(plane, src, c0, c1):
             rows = src.rearrange("g q n -> q g n")
             for quad in range(4):
                 nc.sync.dma_start(
-                    out=plane[32 * quad : 32 * quad + 4, :, c0:c1].bitcast(I32),
+                    out=window(plane, c0, c1)[32 * quad : 32 * quad + 4].bitcast(I32),
                     in_=rows[4 * quad : 4 * quad + 4, :, c0:c1].bitcast(I32),
                 )
 
         def load_x(c0, c1):
             words = x_words.rearrange("g p n t -> p g (n t)")
-            nc.sync.dma_start(out=x_codes[:, :, c0:c1].bitcast(I32), in_=words[:, :, 4 * c0 : 4 * c1].bitcast(I32))
+            nc.sync.dma_start(out=window(x_codes, c0, c1).bitcast(I32), in_=words[:, :, 4 * c0 : 4 * c1].bitcast(I32))
 
         def load_w1(i0, i1):
             words = w1_words.rearrange("g p n -> p g n")
             cols = slice(2 * F * i0, 2 * F * i1)
-            nc.sync.dma_start(out=w1_codes[:, :, cols].bitcast(I32), in_=words[:, :, cols].bitcast(I32))
+            nc.sync.dma_start(out=window(w1_codes, cols.start, cols.stop).bitcast(I32), in_=words[:, :, cols].bitcast(I32))
 
         def load_skip(i):
             nc.sync.dma_start(out=skip_sb[i][:], in_=skip[i].rearrange("(tt p) d -> p tt d", p=P))
 
         def zero(plane, c0, c1):
-            nc.vector.memset(plane[:, :, c0:c1].bitcast(I32), 0)
+            for a, b, tile in plane:
+                if c0 <= a and b <= c1:
+                    nc.vector.memset(tile[:].bitcast(I32), 0)
 
         def identity():
             make_identity(nc, ident[:])
@@ -133,7 +153,7 @@ def tile_mask_hypernetwork_trunk_h2_kernel(
         def il_views(k, c0, c1):
             unit, g = divmod(k, 2)
             i, h = divmod(unit, 2)
-            src = w2_raw[(2 * i + g) % NRAW][:, :, h * HALF + c0 : h * HALF + c1]
+            src = raw_w2(i, g, h * HALF + c0, h * HALF + c1)
             dst = w2_grp[k % NGRP][:, c0:c1, :]
             if FAST:
                 return dst.rearrange("p (c i) t -> p c t i", i=4), src.rearrange("p t (c i) -> p c t i", i=4)
@@ -175,10 +195,10 @@ def tile_mask_hypernetwork_trunk_h2_kernel(
                         for g in range(2):
                             nc.tensor.matmul_mx(
                                 out=bank[:, c0 : c0 + P],
-                                lhsT=w1_codes[:, g, 2 * (i * F + f0) : 2 * (i * F + f0 + P)].bitcast(FP4X4),
-                                lhsT_scale=w1_sc[:, g, i * F + f0 : i * F + f0 + P],
-                                rhs=x_codes[:, g, t0 : t0 + P].bitcast(FP8X4),
-                                rhs_scale=x_sc[:, g, t0 : t0 + P],
+                                lhsT=window(w1_codes, 2 * (i * F + f0), 2 * (i * F + f0 + P))[:, g, :].bitcast(FP4X4),
+                                lhsT_scale=window(w1_sc, i * F + f0, i * F + f0 + P)[:, g, :],
+                                rhs=window(x_codes, t0, t0 + P)[:, g, :].bitcast(FP8X4),
+                                rhs_scale=window(x_sc, t0, t0 + P)[:, g, :],
                                 start=(g == 0),
                                 stop=(g == 1),
                             )
@@ -360,7 +380,7 @@ def tile_mask_hypernetwork_trunk_h2_kernel(
                 i, h = divmod(p, 2)
                 cols = slice(i * TOK, (i + 1) * TOK)
                 nc.vector.quantize_mx(
-                    out=y_codes[:, h, cols].bitcast(FP8X4), scales=y_sc[:, h, cols], in_=y_grp[p % NB][:].bitcast(BF16)
+                    out=y_codes[:, h, cols].bitcast(FP8X4), scales=window(y_sc, cols.start, cols.stop)[:, h, :], in_=y_grp[p % NB][:].bitcast(BF16)
                 )
 
         def store_codes(p):
@@ -375,298 +395,291 @@ def tile_mask_hypernetwork_trunk_h2_kernel(
             for quad in range(4):
                 queue.dma_start(
                     out=rows[4 * quad : 4 * quad + 4, :, c0:c1].bitcast(I32),
-                    in_=y_sc[32 * quad : 32 * quad + 4, :, c0:c1].bitcast(I32),
+                    in_=window(y_sc, c0, c1)[32 * quad : 32 * quad + 4].bitcast(I32),
                 )
 
         identity()
-        vec_zero()
-        load_x(0, 256)
         zero(w1_sc, 0, 1024)
+        load_x(0, 256)
+        vec_load(1)
         vec_load(0)
-        zero(x_sc, 0, 1024)
+        vec_zero()
         zero(w1_sc, 1024, 4096)
         load_scales(w1_sc, w1_scales, 0, 1024)
         load_w1(0, 1)
+        zero(x_sc, 0, 1024)
         load_scales(x_sc, x_scales, 0, 256)
         vec_cast(0)
         load_w2(0, 0, 0, 512)
-        vec_load(1)
+        vec_load(2)
         load_w2(0, 1, 0, 512)
         vec_turn(0)
         vec_copy(0)
+        vec_cast(1)
         load_scales(x_sc, x_scales, 256, 1024)
-        vec_load(2)
+        load_w2(0, 0, 512, 1024)
         mm1(0, 0)
         load_w2(0, 1, 512, 1024)
-        load_w2(0, 0, 512, 1024)
+        load_w2(1, 0, 0, 1024)
+        il_v(0, 448)
         mm1(0, 1)
-        il_v(0, 480)
         relu_h(0, 0)
-        load_scales(w1_sc, w1_scales, 1024, 2048)
-        il_s(0, 480, 512)
-        mm1(1, 0)
-        il_v(1, 496)
+        il_s(0, 448, 512)
         load_w1(1, 2)
-        load_x(256, 512)
+        load_scales(w1_sc, w1_scales, 1024, 2048)
+        mm1(1, 0)
+        il_v(1, 512)
         relu_h(0, 1)
         mm1(1, 1)
-        q_w(0)
         relu_h(1, 0)
+        q_w(0)
+        load_x(256, 512)
         rows_h(0)
-        load_w2(1, 0, 0, 1024)
+        il_v(2, 400)
         relu_h(1, 1)
         rows_h(1)
-        split_h_v(0)
-        vec_cast(1)
+        split_h(0)
         load_w2(1, 1, 0, 1024)
-        il_s(3, 448, 512)
-        load_skip(0)
-        il_v(3, 448)
-        load_scales(w1_sc, w1_scales, 2048, 4096)
+        il_v(3, 416)
         vec_turn(1)
         turn_h(0)
         split_h(1)
-        il_v(2, 432)
-        il_s(1, 496, 512)
-        copy_h(0)
+        il_s(2, 400, 512)
         turn_h(1)
+        copy_h(0)
+        q_w(2)
+        load_skip(0)
         vec_copy(1)
-        q_h(0)
-        load_x(512, 1024)
         copy_h(1)
         q_w(1)
-        il_s(2, 432, 512)
+        il_s(3, 416, 512)
+        q_h(0)
+        load_scales(w1_sc, w1_scales, 2048, 4096)
         q_h(1)
+        il_s(4, 192, 512)
+        il_v(4, 192)
         mm2(0, 0)
+        load_x(512, 1024)
         q_w(3)
-        q_w(2)
         load_w1(2, 3)
-        mm1(2, 0)
-        il_v(4, 400)
-        relu_z(0, 0)
-        mm1(2, 1)
-        il_v(6, 400)
-        relu_h(2, 0)
-        mm1(3, 1)
-        load_w2(2, 0, 0, 1024)
-        relu_h(2, 1)
-        mul_gain(0, 0)
-        mm1(3, 0)
-        il_s(4, 400, 512)
-        rows_h(2)
-        load_w2(2, 1, 0, 1024)
-        relu_h(3, 1)
-        load_w1(3, 4)
-        turn_z(0, 0)
-        q_w(4)
-        load_skip(1)
+        il_v(6, 480)
         mm2(0, 1)
-        relu_h(3, 0)
-        split_h_v(2)
-        il_s(5, 416, 512)
-        rows_h(3)
-        add_skip(0, 0)
-        relu_z(0, 1)
-        il_v(5, 416)
-        turn_h(2)
+        relu_z(0, 0)
         mm2(1, 0)
-        split_h(3)
-        mm2(1, 1)
-        copy_h(2)
-        mul_gain(0, 1)
-        il_v(7, 480)
-        turn_h(3)
-        il_s(6, 400, 512)
-        turn_z(0, 1)
+        mul_gain(0, 0)
+        relu_z(0, 1)
+        mm1(2, 0)
+        q_w(4)
         relu_z(1, 0)
-        mm1(4, 1)
-        load_w2(3, 1, 0, 1024)
-        q_w(6)
-        load_w2(3, 0, 0, 1024)
-        relu_z(1, 1)
-        mm1(4, 0)
+        load_w2(2, 0, 0, 1024)
+        mm1(2, 1)
+        relu_h(2, 0)
         mul_gain(1, 0)
-        il_s(7, 480, 512)
-        q_h(2)
-        copy_h(3)
-        turn_z(1, 0)
-        mul_gain(1, 1)
+        mm1(3, 0)
+        mul_gain(0, 1)
+        load_skip(3)
+        relu_h(2, 1)
+        turn_z(0, 0)
+        il_v(5, 512)
+        rows_h(2)
+        il_s(6, 480, 512)
+        relu_h(3, 0)
+        load_w2(3, 0, 0, 1024)
+        mm1(3, 1)
+        load_w1(3, 4)
+        load_w2(2, 1, 0, 1024)
+        add_skip(0, 0)
+        load_skip(1)
+        split_h(2)
+        q_w(6)
+        turn_z(0, 1)
+        il_s(7, 448, 512)
+        turn_h(2)
+        relu_h(3, 1)
+        mm2(1, 1)
         add_skip(0, 1)
-        relu_h(4, 1)
-        turn_z(1, 1)
+        copy_h(2)
+        il_v(7, 448)
+        rows_h(3)
+        cast_y(0)
+        turn_z(1, 0)
+        mm1(4, 0)
         q_w(5)
+        split_h(3)
+        q_h(2)
+        turn_y(0)
+        relu_z(1, 1)
+        q_w(7)
+        turn_h(3)
+        add_skip(1, 0)
         mm1(5, 0)
         relu_h(4, 0)
-        q_h(3)
-        il_s(10, 480, 512)
-        mm2(2, 0)
-        il_v(8, 464)
-        cast_y(0)
-        rows_h(4)
+        mul_gain(1, 1)
+        copy_h(3)
         il_v(10, 480)
+        turn_z(1, 1)
+        il_s(10, 480, 512)
         relu_h(5, 0)
-        turn_y(0)
-        relu_z(2, 0)
-        mm1(5, 1)
-        add_skip(1, 0)
-        split_h(4)
-        mm2(2, 1)
-        mul_gain(2, 0)
+        mm1(4, 1)
+        q_h(3)
         copy_y(0)
+        mm1(5, 1)
         add_skip(1, 1)
-        turn_z(2, 0)
-        relu_h(5, 1)
-        q_w(7)
-        store_y(1)
-        turn_h(4)
-        il_s(8, 464, 512)
-        il_v(9, 480)
-        rows_h(5)
-        cast_y(1)
-        mm2(3, 0)
-        copy_h(4)
-        add_skip(2, 0)
-        mm1(6, 0)
-        relu_z(2, 1)
+        relu_h(4, 1)
+        mm2(2, 0)
         q_y(0)
-        mm1(7, 0)
-        il_v(11, 480)
-        il_s(11, 480, 512)
+        q_w(10)
+        cast_y(1)
+        rows_h(4)
         store_codes(0)
-        store_y(0)
-        mm1(6, 1)
-        il_s(9, 480, 512)
+        store_y(1)
         load_skip(2)
+        il_v(8, 512)
+        store_y(0)
+        mm2(2, 1)
+        load_w2(3, 1, 0, 1024)
+        relu_h(5, 1)
+        turn_y(1)
+        split_h(4)
+        rows_h(5)
+        il_v(14, 496)
+        relu_z(2, 0)
+        mm2(3, 0)
+        relu_z(2, 1)
+        mm1(6, 0)
+        mul_gain(2, 0)
+        q_w(8)
         split_h(5)
+        mm1(6, 1)
         mul_gain(2, 1)
         relu_z(3, 0)
-        q_w(9)
+        turn_z(2, 0)
+        il_v(9, 512)
+        turn_h(5)
+        copy_y(1)
         turn_z(2, 1)
         relu_h(6, 0)
-        q_w(11)
-        turn_h(5)
+        add_skip(2, 0)
         mm2(3, 1)
-        relu_h(7, 0)
-        mul_gain(3, 0)
-        q_w(8)
-        turn_y(1)
+        il_s(14, 496, 512)
         relu_h(6, 1)
-        mm1(7, 1)
-        q_h(4)
-        copy_h(5)
-        il_v(13, 464)
-        rows_h(6)
-        relu_z(3, 1)
-        turn_z(3, 0)
-        q_h(5)
-        copy_y(1)
-        mm2(4, 1)
         add_skip(2, 1)
-        relu_h(7, 1)
-        mul_gain(3, 1)
-        il_v(12, 432)
+        turn_h(4)
+        mul_gain(3, 0)
+        rows_h(6)
+        copy_h(5)
         store_y(2)
-        split_h(6)
-        turn_z(3, 1)
+        q_w(9)
         cast_y(2)
-        rows_h(7)
-        q_y(1)
-        mm2(4, 0)
-        add_skip(3, 1)
-        il_s(13, 464, 512)
-        turn_h(6)
-        relu_z(4, 1)
-        q_w(10)
+        mm1(7, 0)
+        il_v(11, 512)
+        mm1(7, 1)
+        copy_h(4)
         turn_y(2)
+        il_v(12, 416)
+        split_h(6)
+        turn_z(3, 0)
+        relu_z(3, 1)
+        turn_h(6)
+        q_h(4)
+        relu_h(7, 0)
+        q_h(5)
+        mul_gain(3, 1)
+        mm2(4, 0)
+        relu_h(7, 1)
         add_skip(3, 0)
+        turn_z(3, 1)
+        il_s(12, 416, 512)
+        il_v(13, 512)
+        rows_h(7)
         relu_z(4, 0)
-        mm2(5, 1)
-        il_v(15, 464)
-        il_s(12, 432, 512)
-        store_y(3)
-        mm2(5, 0)
-        load_skip(3)
-        split_h(7)
-        store_codes(1)
-        copy_y(2)
-        mul_gain(4, 1)
-        mul_gain(4, 0)
+        mm2(4, 1)
         copy_h(6)
-        turn_z(4, 1)
-        il_v(14, 432)
-        turn_h(7)
-        cast_y(3)
+        add_skip(3, 1)
+        copy_y(2)
+        mul_gain(4, 0)
+        store_y(3)
+        q_w(11)
+        relu_z(4, 1)
         turn_z(4, 0)
+        il_v(15, 464)
+        mm2(5, 1)
+        mul_gain_s(4, 1)
+        cast_y(3)
+        turn_z(4, 1)
+        add_skip(4, 0)
         q_h(6)
-        q_w(13)
-        copy_h(7)
+        split_h(7)
+        add_skip(4, 1)
         turn_y(3)
         il_s(15, 464, 512)
+        q_y(1)
+        turn_h(7)
+        copy_y(3)
+        q_w(13)
+        mm2(5, 0)
+        store_codes(1)
+        store_y(4)
+        copy_h(7)
         q_w(12)
-        relu_z(5, 1)
-        add_skip(4, 0)
-        relu_z(5, 0)
+        cast_y(4)
         q_h(7)
         mm2(6, 1)
-        mul_gain(5, 1)
-        il_s(14, 432, 512)
-        add_skip(4, 1)
-        copy_y(3)
-        mul_gain(5, 0)
-        mm2(6, 0)
-        q_w(14)
-        store_y(4)
-        cast_y(4)
-        turn_z(5, 1)
-        q_w(15)
-        turn_z(5, 0)
-        relu_z(6, 0)
         q_y(3)
-        turn_y(4)
-        add_skip(5, 1)
-        relu_z(6, 1)
-        mm2(7, 0)
-        add_skip(5, 0)
-        mm2(7, 1)
-        copy_y(4)
-        mul_gain(6, 0)
-        cast_y_v(5)
-        store_y(5)
-        mul_gain_s(6, 1)
-        turn_z(6, 0)
-        q_y(2)
-        relu_z(7, 0)
-        q_y(4)
-        turn_y(5)
-        add_skip(6, 0)
-        turn_z(6, 1)
-        relu_z(7, 1)
-        store_codes(4)
-        store_codes(2)
-        mul_gain(7, 0)
+        q_w(14)
+        relu_z(5, 0)
         store_codes(3)
-        add_skip(6, 1)
+        turn_y(4)
+        q_y(2)
+        relu_z(5, 1)
+        mm2(6, 0)
+        mul_gain(5, 0)
+        q_w(15)
+        copy_y(4)
+        turn_z(5, 0)
+        mul_gain(5, 1)
+        relu_z(6, 0)
+        mm2(7, 0)
+        q_y(4)
+        add_skip(5, 0)
+        relu_z(6, 1)
+        turn_z(5, 1)
+        store_codes(4)
+        mul_gain(6, 0)
+        mm2(7, 1)
+        relu_z(7, 0)
+        add_skip(5, 1)
+        turn_z(6, 0)
+        mul_gain_s(7, 0)
+        mul_gain(6, 1)
+        store_y(5)
+        cast_y_v(5)
+        relu_z(7, 1)
+        store_codes(2)
+        turn_z(6, 1)
+        add_skip(6, 0)
         turn_z(7, 0)
-        mul_gain(7, 1)
+        mul_gain_s(7, 1)
+        turn_y(5)
+        add_skip(6, 1)
+        turn_z(7, 1)
+        copy_y(5)
+        add_skip_bf(7, 0)
         store_y(6)
         cast_y(6)
-        add_skip(7, 0)
-        turn_z(7, 1)
-        add_skip_bf(7, 0)
-        store_y_half(7, 0)
-        copy_y(5)
         add_skip_bf(7, 1)
-        turn_y(6)
         q_y(5)
         turn_y(7)
-        add_skip(7, 1)
-        copy_y(6)
-        store_scales(0, 768)
-        copy_y(7)
+        add_skip(7, 0)
         store_codes(5)
-        store_y_half(7, 1)
-        q_y(6)
+        store_scales(0, 768)
+        turn_y(6)
+        add_skip(7, 1)
+        copy_y(7)
+        store_y(7)
+        copy_y(6)
         q_y(7)
-        store_codes(6)
+        q_y(6)
         store_codes(7)
+        store_codes(6)
         store_scales(768, 1024)

from contextlib import ExitStack

import concourse.mybir as mybir
from concourse.masks import make_identity

F32 = mybir.dt.float32
BF16 = mybir.dt.bfloat16
I32 = mybir.dt.int32
U32 = mybir.dt.uint32
U8 = mybir.dt.uint8
FP8X4 = mybir.dt.float8_e4m3fn_x4
FP4X4 = mybir.dt.float4_e2m1fn_x4
ALU = mybir.AluOpType
ACT = mybir.ActivationFunctionType

NETS, TOK, D, F = 4, 256, 1024, 1024
FLOPS = 2 * NETS * TOK * D * F * 2
P = 128
HALF = 512
UNITS = 2 * NETS
VCOLS = 288
NGRP = 4
NWQ = 6
NY = 5
NRAW = 4
NHQ = 4
NB = 3
NBANK = 8
NZ = 3
FAST = True
WA = 3


def tile_mask_hypernetwork_trunk_h2_kernel(
    tc, x_words, x_scales, w1_words, w1_scales, b1, w2, b2, gain, skip, out_0, out_1, out_2
):
    nc = tc.nc
    with ExitStack() as ctx:
        sb = ctx.enter_context(tc.tile_pool(name="sb", bufs=1))
        ps = ctx.enter_context(tc.psum_pool(name="ps", bufs=1))
        ctx.enter_context(tc.manual_schedule())

        def tiles(name, count, shape, dtype):
            return [sb.tile(shape, dtype, name="%s%d" % (name, n), align_bytes=64) for n in range(count)]

        def banks(name, count):
            return [ps.tile([P, HALF], F32, name="%s%d" % (name, n)) for n in range(count)]

        (ident,) = tiles("ident", 1, [P, P], F32)
        (ident_bf,) = tiles("ident_bf", 1, [P, P], BF16)
        (vec_bf,) = tiles("vec_bf", 1, [96, P], BF16)
        (vec_rows,) = tiles("vec_rows", 1, [P, P], F32)
        (b1_cols,) = tiles("b1_cols", 1, [P, 32], F32)
        (out_cols,) = tiles("out_cols", 1, [P, 64], F32)
        def pieces(name, cuts, dtype):
            return [
                (c0, c1, sb.tile([P, 2, c1 - c0], dtype, name="%s%d" % (name, c0), align_bytes=64))
                for c0, c1 in zip(cuts, cuts[1:])
            ]

        def window(parts, c0, c1):
            ((a, tile),) = [(a, tile) for a, b, tile in parts if a <= c0 and c1 <= b]
            return tile[:, :, c0 - a : c1 - a]

        x_codes = pieces("x_codes", (0, 256, 512, 1024), U32)
        x_sc = pieces("x_sc", (0, 256, 1024), U8)
        w1_codes = pieces("w1_codes", (0, 2048, 4096, 6144, 8192), U8)
        w1_sc = pieces("w1_sc", (0, 1024, 2048, 4096), U8)
        w2_first = tiles("w2_first", 4, [P, 4, HALF], BF16)
        w2_raw = tiles("w2_raw", NRAW, [P, 4, D], BF16)

        def raw_w2(i, g, c0, c1):
            if i == 0:
                h = c0 // HALF
                return w2_first[2 * h + g][:, :, c0 - h * HALF : c1 - h * HALF]
            return w2_raw[(2 * i + g - 2) % NRAW][:, :, c0:c1]

        skip_sb = tiles("skip_sb", NETS, [P, 2, D], BF16)
        w2_grp = tiles("w2_grp", NGRP, [P, HALF, 4], BF16)
        w2_codes = tiles("w2_codes", NWQ, [P, 2, HALF], U32)
        w2_sc = tiles("w2_sc", NWQ, [P, 2, HALF], U8)
        h_rows = tiles("h_rows", NB, [P, 2, 2, 2 * P], BF16)
        h_cols = tiles("h_cols", NB, [P, 4, TOK], BF16)
        h_grp = tiles("h_grp", NB, [P, 2 * TOK], F32)
        h_codes = tiles("h_codes", NHQ, [P, 2, TOK], U32)
        h_sc = tiles("h_sc", NHQ, [P, 2, TOK], U8)
        z_cols = tiles("z_cols", NZ, [P, 4, TOK], F32)
        y_rows = tiles("y_rows", NY, [P, 2, HALF], F32)
        y_bf = tiles("y_bf", NB, [P, 2, 2, 2 * P], BF16)
        y_grp = tiles("y_grp", NB, [P, 2 * TOK], F32)
        (y_codes,) = tiles("y_codes", 1, [P, 2, NETS * TOK], U32)
        y_sc = pieces("y_sc", (0, 768, 1024), U8)

        psum = banks("bank", NBANK)
        bank_of = {}

        def take_bank(*key):
            bank_of[key] = psum[len(bank_of) % NBANK]
            return bank_of[key]

        def load_w2(i, g, c0, c1):
            rows = w2[i, g * HALF : (g + 1) * HALF, :].rearrange("(p j) d -> p j d", j=4)
            nc.sync.dma_start(out=raw_w2(i, g, c0, c1), in_=rows[:, :, c0:c1])

        def load_scales(plane, src, c0, c1):
            rows = src.rearrange("g q n -> q g n")
            for quad in range(4):
                nc.sync.dma_start(
                    out=window(plane, c0, c1)[32 * quad : 32 * quad + 4].bitcast(I32),
                    in_=rows[4 * quad : 4 * quad + 4, :, c0:c1].bitcast(I32),
                )

        def load_x(c0, c1):
            words = x_words.rearrange("g p n t -> p g (n t)")
            nc.sync.dma_start(out=window(x_codes, c0, c1).bitcast(I32), in_=words[:, :, 4 * c0 : 4 * c1].bitcast(I32))

        def load_w1(i0, i1):
            words = w1_words.rearrange("g p n -> p g n")
            cols = slice(2 * F * i0, 2 * F * i1)
            nc.sync.dma_start(out=window(w1_codes, cols.start, cols.stop).bitcast(I32), in_=words[:, :, cols].bitcast(I32))

        def load_skip(i):
            nc.sync.dma_start(out=skip_sb[i][:], in_=skip[i].rearrange("(tt p) d -> p tt d", p=P))

        def zero(plane, c0, c1):
            for a, b, tile in plane:
                if c0 <= a and b <= c1:
                    nc.vector.memset(tile[:].bitcast(I32), 0)

        def identity():
            make_identity(nc, ident[:])
            make_identity(nc, ident_bf[:])

        def vec_zero():
            nc.vector.memset(vec_rows[:], 0.0)

        def vec_load(n):
            src = (b1, b2, gain)[n]
            nc.sync.dma_start(out=vec_bf[32 * n : 32 * n + 32, :], in_=src.rearrange("t (c n) -> (t c) n", n=P))

        def vec_cast(s):
            for n in ((0,), (1, 2))[s]:
                rows = slice(32 * n, 32 * n + 32)
                nc.scalar.activation(out=vec_rows[rows, :], in_=vec_bf[rows, :], func=ACT.Identity)

        def vec_turn(s):
            nc.tensor.transpose(take_bank("vec", s)[:, 0:P], vec_rows[:], ident[:])

        def vec_copy(s):
            cols = (slice(0, 32), slice(32, 96))[s]
            nc.scalar.copy(out=(b1_cols, out_cols)[s][:], in_=bank_of[("vec", s)][:, cols])

        def il_views(k, c0, c1):
            unit, g = divmod(k, 2)
            i, h = divmod(unit, 2)
            src = raw_w2(i, g, h * HALF + c0, h * HALF + c1)
            dst = w2_grp[k % NGRP][:, c0:c1, :]
            if FAST:
                return dst.rearrange("p (c i) t -> p c t i", i=4), src.rearrange("p t (c i) -> p c t i", i=4)
            return dst, src.rearrange("p t c -> p c t")

        def il_v(k, c):
            if 0 <= k < 2 * UNITS:
                dst, src = il_views(k, 0, c)
                nc.vector.tensor_copy(out=dst, in_=src)

        def il_s(k, c, c1=HALF):
            if c < c1:
                dst, src = il_views(k, c, c1)
                nc.scalar.copy(out=dst, in_=src)

        def il_p(k, c):
            if 0 <= k < 2 * UNITS:
                dst, src = il_views(k, c, HALF)
                nc.gpsimd.tensor_scalar(out=dst, in0=src, scalar1=1.0, scalar2=0.0, op0=ALU.mult, op1=ALU.add)

        def q_w(k):
            if 0 <= k < 2 * UNITS:
                unit, g = divmod(k, 2)
                nc.vector.quantize_mx(
                    out=w2_codes[unit % NWQ][:, g, :].bitcast(FP8X4),
                    scales=w2_sc[unit % NWQ][:, g, :],
                    in_=w2_grp[k % NGRP][:].rearrange("p c t -> p (c t)"),
                )

        def mm1(q, s):
            if 0 <= q < UNITS:
                i, fh = divmod(q, 2)
                bank = take_bank("h", q, s)
                for fl in range(2):
                    f0 = fh * HALF + (2 * s + fl) * P
                    for tt in range(2):
                        t0 = i * TOK + tt * P
                        c0 = fl * TOK + tt * P
                        for g in range(2):
                            nc.tensor.matmul_mx(
                                out=bank[:, c0 : c0 + P],
                                lhsT=window(w1_codes, 2 * (i * F + f0), 2 * (i * F + f0 + P))[:, g, :].bitcast(FP4X4),
                                lhsT_scale=window(w1_sc, i * F + f0, i * F + f0 + P)[:, g, :],
                                rhs=window(x_codes, t0, t0 + P)[:, g, :].bitcast(FP8X4),
                                rhs_scale=window(x_sc, t0, t0 + P)[:, g, :],
                                start=(g == 0),
                                stop=(g == 1),
                            )

        def relu_h(q, s):
            if 0 <= q < UNITS:
                for fl in range(2):
                    c = 4 * q + 2 * s + fl
                    nc.scalar.activation(
                        out=h_cols[q % NB][:, 2 * s + fl, :],
                        in_=bank_of[("h", q, s)][:, fl * TOK : (fl + 1) * TOK],
                        func=ACT.Relu,
                        bias=b1_cols[:, c : c + 1],
                    )

        def rows_h(q):
            if 0 <= q < UNITS:
                bank = take_bank("rows", q)
                for tt in range(2):
                    for fl in range(4):
                        c0 = tt * HALF + fl * P
                        nc.tensor.transpose(
                            bank[:].bitcast(BF16)[:, c0 : c0 + P],
                            h_cols[q % NB][:, fl, tt * P : (tt + 1) * P],
                            ident_bf[:],
                        )

        def split_h(q):
            if 0 <= q < UNITS:
                nc.scalar.copy(
                    out=h_rows[q % NB][:].rearrange("p u tt w -> p u (tt w)").bitcast(F32),
                    in_=bank_of[("rows", q)][:].rearrange("p (w u) -> p u w", u=2),
                )

        def turn_words(bank, rows):
            for tt in range(2):
                for u in range(2):
                    c0 = u * TOK + tt * P
                    nc.tensor.transpose(bank[:, c0 : c0 + P], rows[:, u, tt, :].bitcast(F32), ident[:])

        def split_h_v(q):
            nc.vector.tensor_copy(
                out=h_rows[q % NB][:].rearrange("p u tt w -> p u (tt w)").bitcast(F32),
                in_=bank_of[("rows", q)][:].rearrange("p (w u) -> p u w", u=2),
            )

        def turn_h(q):
            if 0 <= q < UNITS:
                turn_words(take_bank("hw", q), h_rows[q % NB])

        def copy_h(q):
            if 0 <= q < UNITS:
                nc.scalar.copy(
                    out=h_grp[q % NB][:].rearrange("p (r u) -> p r u", u=2),
                    in_=bank_of[("hw", q)][:].rearrange("p (u r) -> p r u", u=2),
                )

        def q_h(q):
            if 0 <= q < UNITS:
                i, fh = divmod(q, 2)
                nc.vector.quantize_mx(
                    out=h_codes[i % NHQ][:, fh, :].bitcast(FP8X4), scales=h_sc[i % NHQ][:, fh, :], in_=h_grp[q % NB][:].bitcast(BF16)
                )

        def mm2(p, z):
            if 0 <= p < UNITS:
                i = p // 2
                bank = take_bank("z", p, z)
                for dl in range(2):
                    d0 = (2 * z + dl) * P
                    for g in range(2):
                        nc.tensor.matmul_mx(
                            out=bank[:, dl * TOK : (dl + 1) * TOK],
                            lhsT=w2_codes[p % NWQ][:, g, d0 : d0 + P].bitcast(FP8X4),
                            lhsT_scale=w2_sc[p % NWQ][:, g, d0 : d0 + P],
                            rhs=h_codes[i % NHQ][:, g, :].bitcast(FP8X4),
                            rhs_scale=h_sc[i % NHQ][:, g, :],
                            start=(g == 0),
                            stop=(g == 1),
                        )

        def relu_z(p, z):
            if 0 <= p < UNITS:
                for dl in range(2):
                    c = 4 * p + 2 * z + dl
                    nc.scalar.activation(
                        out=z_cols[p % NZ][:, 2 * z + dl, :],
                        in_=bank_of[("z", p, z)][:, dl * TOK : (dl + 1) * TOK],
                        func=ACT.Relu,
                        bias=out_cols[:, c : c + 1],
                    )

        def mul_gain(p, z):
            if 0 <= p < UNITS:
                for dl in range(2):
                    c = 32 + 4 * p + 2 * z + dl
                    zc = z_cols[p % NZ][:, 2 * z + dl, :]
                    nc.vector.tensor_scalar(
                        out=zc, in0=zc, scalar1=out_cols[:, c : c + 1], scalar2=None, op0=ALU.mult
                    )

        def mul_gain_s(p, z):
            for dl in range(2):
                c = 32 + 4 * p + 2 * z + dl
                zc = z_cols[p % NZ][:, 2 * z + dl, :]
                nc.scalar.activation(out=zc, in_=zc, func=ACT.Copy, scale=out_cols[:, c : c + 1])

        def turn_z(p, z):
            if 0 <= p < UNITS:
                bank = take_bank("zt", p, z)
                for tt in range(2):
                    for dl in range(2):
                        c0 = tt * TOK + dl * P
                        nc.tensor.transpose(
                            bank[:, c0 : c0 + P], z_cols[p % NZ][:, 2 * z + dl, tt * P : (tt + 1) * P], ident[:]
                        )

        def add_skip(p, z):
            if 0 <= p < UNITS:
                i, h = divmod(p, 2)
                d0 = h * HALF + z * 256
                nc.vector.tensor_tensor(
                    out=y_rows[p % NY][:, :, z * 256 : (z + 1) * 256],
                    in0=bank_of[("zt", p, z)][:].rearrange("p (tt d) -> p tt d", tt=2),
                    in1=skip_sb[i][:, :, d0 : d0 + 256],
                    op=ALU.add,
                )

        def add_skip_bf(p, z):
            i, h = divmod(p, 2)
            d0 = h * HALF + z * 256
            for tt in range(2):
                nc.vector.tensor_tensor(
                    out=y_bf[p % NB][:, :, tt, z * P : (z + 1) * P].rearrange("p u (w e) -> p u w e", e=2),
                    in0=bank_of[("zt", p, z)][:, tt * TOK : (tt + 1) * TOK].rearrange("p (w u e) -> p u w e", u=2, e=2),
                    in1=skip_sb[i][:, tt, d0 : d0 + 256].rearrange("p (w u e) -> p u w e", u=2, e=2),
                    op=ALU.add,
                )

        def store_y(p):
            if 0 <= p < UNITS:
                i, h = divmod(p, 2)
                dst = out_0[i].rearrange("(tt p) d -> p tt d", p=P)[:, :, h * HALF : (h + 1) * HALF]
                nc.sync.dma_start(out=dst, in_=y_rows[p % NY][:])

        def store_y_half(p, z):
            i, h = divmod(p, 2)
            d0 = h * HALF + z * 256
            dst = out_0[i].rearrange("(tt p) d -> p tt d", p=P)[:, :, d0 : d0 + 256]
            nc.sync.dma_start(out=dst, in_=y_rows[p % NY][:, :, z * 256 : (z + 1) * 256])

        def cast_views(p):
            dst = y_bf[p % NB][:].rearrange("p u tt (w e) -> p u (tt w) e", e=2)
            return dst, y_rows[p % NY][:].rearrange("p tt (w u e) -> p u (tt w) e", u=2, e=2)

        def cast_y(p):
            if 0 <= p < UNITS:
                dst, src = cast_views(p)
                nc.scalar.copy(out=dst, in_=src)

        def cast_y_v(p):
            if 0 <= p < UNITS:
                dst, src = cast_views(p)
                nc.vector.tensor_copy(out=dst, in_=src)

        def turn_y(p):
            if 0 <= p < UNITS:
                turn_words(take_bank("yw", p), y_bf[p % NB])

        def copy_y(p):
            if 0 <= p < UNITS:
                nc.scalar.copy(
                    out=y_grp[p % NB][:].rearrange("p (r u) -> p r u", u=2),
                    in_=bank_of[("yw", p)][:].rearrange("p (u r) -> p r u", u=2),
                )

        def q_y(p):
            if 0 <= p < UNITS:
                i, h = divmod(p, 2)
                cols = slice(i * TOK, (i + 1) * TOK)
                nc.vector.quantize_mx(
                    out=y_codes[:, h, cols].bitcast(FP8X4), scales=window(y_sc, cols.start, cols.stop)[:, h, :], in_=y_grp[p % NB][:].bitcast(BF16)
                )

        def store_codes(p):
            if 0 <= p < UNITS:
                i, h = divmod(p, 2)
                dst = out_1[h].rearrange("p m t -> p (m t)")[:, 4 * i * TOK : 4 * (i + 1) * TOK]
                nc.sync.dma_start(out=dst.bitcast(I32), in_=y_codes[:, h, i * TOK : (i + 1) * TOK].bitcast(I32))

        def store_scales(c0, c1):
            rows = out_2.rearrange("g q m -> q g m")
            queue = nc.sync if c0 == 0 else nc.scalar
            for quad in range(4):
                queue.dma_start(
                    out=rows[4 * quad : 4 * quad + 4, :, c0:c1].bitcast(I32),
                    in_=window(y_sc, c0, c1)[32 * quad : 32 * quad + 4].bitcast(I32),
                )

        identity()
        zero(w1_sc, 0, 1024)
        load_x(0, 256)
        vec_load(1)
        vec_load(0)
        vec_zero()
        zero(w1_sc, 1024, 4096)
        load_scales(w1_sc, w1_scales, 0, 1024)
        load_w1(0, 1)
        zero(x_sc, 0, 1024)
        load_scales(x_sc, x_scales, 0, 256)
        vec_cast(0)
        load_w2(0, 0, 0, 512)
        vec_load(2)
        load_w2(0, 1, 0, 512)
        vec_turn(0)
        vec_copy(0)
        vec_cast(1)
        load_scales(x_sc, x_scales, 256, 1024)
        load_w2(0, 0, 512, 1024)
        mm1(0, 0)
        load_w2(0, 1, 512, 1024)
        load_w2(1, 0, 0, 1024)
        il_v(0, 448)
        mm1(0, 1)
        relu_h(0, 0)
        il_s(0, 448, 512)
        load_w1(1, 2)
        load_scales(w1_sc, w1_scales, 1024, 2048)
        mm1(1, 0)
        il_v(1, 512)
        relu_h(0, 1)
        mm1(1, 1)
        relu_h(1, 0)
        q_w(0)
        load_x(256, 512)
        rows_h(0)
        il_v(2, 400)
        relu_h(1, 1)
        rows_h(1)
        split_h(0)
        load_w2(1, 1, 0, 1024)
        il_v(3, 416)
        vec_turn(1)
        turn_h(0)
        split_h(1)
        il_s(2, 400, 512)
        turn_h(1)
        copy_h(0)
        q_w(2)
        load_skip(0)
        vec_copy(1)
        copy_h(1)
        q_w(1)
        il_s(3, 416, 512)
        q_h(0)
        load_scales(w1_sc, w1_scales, 2048, 4096)
        q_h(1)
        il_s(4, 192, 512)
        il_v(4, 192)
        mm2(0, 0)
        load_x(512, 1024)
        q_w(3)
        load_w1(2, 3)
        il_v(6, 480)
        mm2(0, 1)
        relu_z(0, 0)
        mm2(1, 0)
        mul_gain(0, 0)
        relu_z(0, 1)
        mm1(2, 0)
        q_w(4)
        relu_z(1, 0)
        load_w2(2, 0, 0, 1024)
        mm1(2, 1)
        relu_h(2, 0)
        mul_gain(1, 0)
        mm1(3, 0)
        mul_gain(0, 1)
        load_skip(3)
        relu_h(2, 1)
        turn_z(0, 0)
        il_v(5, 512)
        rows_h(2)
        il_s(6, 480, 512)
        relu_h(3, 0)
        load_w2(3, 0, 0, 1024)
        mm1(3, 1)
        load_w1(3, 4)
        load_w2(2, 1, 0, 1024)
        add_skip(0, 0)
        load_skip(1)
        split_h(2)
        q_w(6)
        turn_z(0, 1)
        il_s(7, 448, 512)
        turn_h(2)
        relu_h(3, 1)
        mm2(1, 1)
        add_skip(0, 1)
        copy_h(2)
        il_v(7, 448)
        rows_h(3)
        cast_y(0)
        turn_z(1, 0)
        mm1(4, 0)
        q_w(5)
        split_h(3)
        q_h(2)
        turn_y(0)
        relu_z(1, 1)
        q_w(7)
        turn_h(3)
        add_skip(1, 0)
        mm1(5, 0)
        relu_h(4, 0)
        mul_gain(1, 1)
        copy_h(3)
        il_v(10, 480)
        turn_z(1, 1)
        il_s(10, 480, 512)
        relu_h(5, 0)
        mm1(4, 1)
        q_h(3)
        copy_y(0)
        mm1(5, 1)
        add_skip(1, 1)
        relu_h(4, 1)
        mm2(2, 0)
        q_y(0)
        q_w(10)
        cast_y(1)
        rows_h(4)
        store_codes(0)
        store_y(1)
        load_skip(2)
        il_v(8, 512)
        store_y(0)
        mm2(2, 1)
        load_w2(3, 1, 0, 1024)
        relu_h(5, 1)
        turn_y(1)
        split_h(4)
        rows_h(5)
        il_v(14, 496)
        relu_z(2, 0)
        mm2(3, 0)
        relu_z(2, 1)
        mm1(6, 0)
        mul_gain(2, 0)
        q_w(8)
        split_h(5)
        mm1(6, 1)
        mul_gain(2, 1)
        relu_z(3, 0)
        turn_z(2, 0)
        il_v(9, 512)
        turn_h(5)
        copy_y(1)
        turn_z(2, 1)
        relu_h(6, 0)
        add_skip(2, 0)
        mm2(3, 1)
        il_s(14, 496, 512)
        relu_h(6, 1)
        add_skip(2, 1)
        turn_h(4)
        mul_gain(3, 0)
        rows_h(6)
        copy_h(5)
        store_y(2)
        q_w(9)
        cast_y(2)
        mm1(7, 0)
        il_v(11, 512)
        mm1(7, 1)
        copy_h(4)
        turn_y(2)
        il_v(12, 416)
        split_h(6)
        turn_z(3, 0)
        relu_z(3, 1)
        turn_h(6)
        q_h(4)
        relu_h(7, 0)
        q_h(5)
        mul_gain(3, 1)
        mm2(4, 0)
        relu_h(7, 1)
        add_skip(3, 0)
        turn_z(3, 1)
        il_s(12, 416, 512)
        il_v(13, 512)
        rows_h(7)
        relu_z(4, 0)
        mm2(4, 1)
        copy_h(6)
        add_skip(3, 1)
        copy_y(2)
        mul_gain(4, 0)
        store_y(3)
        q_w(11)
        relu_z(4, 1)
        turn_z(4, 0)
        il_v(15, 464)
        mm2(5, 1)
        mul_gain_s(4, 1)
        cast_y(3)
        turn_z(4, 1)
        add_skip(4, 0)
        q_h(6)
        split_h(7)
        add_skip(4, 1)
        turn_y(3)
        il_s(15, 464, 512)
        q_y(1)
        turn_h(7)
        copy_y(3)
        q_w(13)
        mm2(5, 0)
        store_codes(1)
        store_y(4)
        copy_h(7)
        q_w(12)
        cast_y(4)
        q_h(7)
        mm2(6, 1)
        q_y(3)
        q_w(14)
        relu_z(5, 0)
        store_codes(3)
        turn_y(4)
        q_y(2)
        relu_z(5, 1)
        mm2(6, 0)
        mul_gain(5, 0)
        q_w(15)
        copy_y(4)
        turn_z(5, 0)
        mul_gain(5, 1)
        relu_z(6, 0)
        mm2(7, 0)
        q_y(4)
        add_skip(5, 0)
        relu_z(6, 1)
        turn_z(5, 1)
        store_codes(4)
        mul_gain(6, 0)
        mm2(7, 1)
        relu_z(7, 0)
        add_skip(5, 1)
        turn_z(6, 0)
        mul_gain_s(7, 0)
        mul_gain(6, 1)
        store_y(5)
        cast_y_v(5)
        relu_z(7, 1)
        store_codes(2)
        turn_z(6, 1)
        add_skip(6, 0)
        turn_z(7, 0)
        mul_gain_s(7, 1)
        turn_y(5)
        add_skip(6, 1)
        turn_z(7, 1)
        copy_y(5)
        add_skip_bf(7, 0)
        store_y(6)
        cast_y(6)
        add_skip_bf(7, 1)
        q_y(5)
        turn_y(7)
        add_skip(7, 0)
        store_codes(5)
        store_scales(0, 768)
        turn_y(6)
        add_skip(7, 1)
        copy_y(7)
        store_y(7)
        copy_y(6)
        q_y(7)
        q_y(6)
        store_codes(7)
        store_codes(6)
        store_scales(768, 1024)
